import numpy as np
import ml_dtypes


def mxq(x, axis, fmt="e4m3"):
    dtype, down = {"e4m3": (ml_dtypes.float8_e4m3fn, 7), "e5m2": (ml_dtypes.float8_e5m2, 14)}[fmt]
    v = np.moveaxis(np.asarray(x, np.float32).astype(ml_dtypes.bfloat16).astype(np.float64), axis, -1)
    blocks = v.reshape(v.shape[:-1] + (-1, 32))
    amax = np.abs(blocks).max(-1, keepdims=True)
    byte = np.maximum(np.where(amax > 0, np.frexp(amax)[1] - 1 + 127, 0) - down, 1)
    scale = np.exp2(byte - 127.0)
    codes = (blocks / scale).astype(np.float32).astype(dtype).astype(np.float64)
    return np.moveaxis((codes * scale).reshape(v.shape), -1, axis)


WIDE = False


def mx_kscale(k):
    if not WIDE:
        return np.ones(k)
    levels = np.array([18, -18])
    if k % 512:
        return np.exp2(np.random.permutation(np.resize(levels, k // 32))).repeat(32)
    a = np.empty((k // 512, 16))
    for p in range(k // 512):
        a[p, :8] = np.random.permutation(np.resize(levels, 8))
        for g in range(8):
            far = levels[np.abs(levels - a[p, g]) >= 10]
            a[p, g + 8] = far[np.random.randint(len(far))]
    return np.exp2(a.ravel()).repeat(32)


def f64(x):
    return np.asarray(x).astype(np.float64)


def striped(idx):
    return np.tile(np.asarray(idx).reshape(-1, 16).T, (8, 1)).astype(np.uint16)


def unstriped(offs):
    return offs[:16].T.reshape(-1).astype(np.int64)


def setup_inputs():
    n = np.random.standard_normal
    uni = np.random.uniform
    order = np.random.permutation(2048)
    neg = order[:512]
    pos = order[512:1024]
    f_d = mx_kscale(512)
    f_i = np.ones(2048)
    f_i[neg] = mx_kscale(512)
    return {
        "x": (0.5 * n((512, 512)) * f_d[None, :]).astype(np.float32),
        "wT": (n((512, 2048)) / np.sqrt(512) / f_d[:, None] * f_i[None, :]).astype(np.float32),
        "us": (uni(0.75, 1.3, (512, 1))).astype(np.float32),
        "ts": np.tile(uni(0.75, 1.3, 2048) / f_i, (128, 1)).astype(np.float32),
        "wt": (uni(0.75, 1.3, (512, 1))).astype(np.float32),
        "offs": striped(neg),
        "poffs": striped(pos),
    }


def reference(x, wT, us, ts, wt, offs, poffs):
    neg = unstriped(offs)
    pos = unstriped(poffs)
    wT_i = f64(wT)[:, neg]
    wT_r = f64(wT)[:, pos]
    ts_i = f64(ts)[:1][:, neg]
    ts_r = f64(ts)[:1][:, pos]
    tpc = ts_r.T
    wpr = wT_r.T
    s0 = (f64(x) * wpr).sum(-1, keepdims=True)
    sp = f64(us) * tpc * s0
    a = mxq(f64(x), 1, "e4m3") @ mxq(wT_i, 0, "e4m3")
    z = f64(us) * ts_i * a
    m0 = (z).max(-1, keepdims=True)
    m = np.maximum(m0, sp)
    e = np.exp(z - m)
    ep = np.exp(sp - m)
    tot0 = (e).sum(-1, keepdims=True)
    inv = 1.0 / (tot0 + ep)
    g = f64(wt) * f64(us) * ts_i * e * inv
    gp = f64(wt) * f64(us) * tpc * (ep * inv - 1.0)
    gx = mxq(g, 1, "e5m2") @ mxq(wT_i, 1, "e4m3").T
    out = gx + gp * wpr
    return out

@@ -1,0 +1,294 @@
+from contextlib import ExitStack
+
+import concourse.mybir as mybir
+from concourse.masks import make_identity
+
+R, D, T, I = 512, 512, 2048, 512
+FLOPS = 2 * 2 * R * D * I
+
+F32 = mybir.dt.float32
+BF16 = mybir.dt.bfloat16
+U32 = mybir.dt.uint32
+U16 = mybir.dt.uint16
+U8 = mybir.dt.uint8
+E4M3 = mybir.dt.float8_e4m3fn_x4
+E5M2 = mybir.dt.float8_e5m2_x4
+ALU = mybir.AluOpType
+ACT = mybir.ActivationFunctionType
+
+P = 128
+PACK = 4
+TILES = 4
+HALF = 256
+LAST = P - 1
+ORDER = [("w", 0), ("x", 0), ("x", 1), ("w", 1), ("x", 2), ("w", 2), ("x", 3), ("w", 3)]
+
+
+def tile_attend_gspos_sm_x_kernel(tc, x, wT, us, ts, wt, offs, poffs, out):
+    nc = tc.nc
+    with ExitStack() as ctx:
+        keep = ctx.enter_context(tc.tile_pool(name="keep", bufs=1))
+        psum = ctx.enter_context(tc.psum_pool(name="psum", bufs=1))
+
+        neg_list = keep.tile([P, I // 16], U16, name="neg_list")
+        pos_list = keep.tile([P, R // 16], U16, name="pos_list")
+        ts_table = keep.tile([P, T], F32, name="ts_table")
+        row_factors = keep.tile([P, R], F32, name="row_factors")
+        planes = [keep.tile([P, T], F32, name=f"plane{t}") for t in range(PACK)]
+        x_rows = [keep.tile([P, D], F32, name=f"x_rows{j}") for j in range(TILES)]
+        ident = keep.tile([P, P], F32, name="ident")
+        warm = keep.tile([P, 1], F32, name="warm")
+        warm2 = keep.tile([P, 1], F32, name="warm2")
+
+        wT_planes = wT.rearrange("(b t q) c -> t b q c", t=PACK, q=8)
+        nc.sync.dma_start(neg_list[:], offs)
+        nc.sync.dma_start(ts_table[LAST:P, :], ts[0:1, :])
+        nc.sync.dma_start(pos_list[:], poffs)
+        for kind, n in ORDER:
+            if kind == "w":
+                nc.sync.dma_start(planes[n][:], wT_planes[n])
+            else:
+                nc.sync.dma_start(x_rows[n][:], x[n * P:(n + 1) * P, :])
+        nc.scalar.dma_start(row_factors[LAST - 1:LAST, :], us.rearrange("r o -> o r"))
+        nc.scalar.dma_start(row_factors[LAST:P, :], wt.rearrange("r o -> o r"))
+
+        nc.vector.memset(warm[:], 0.0)
+        nc.vector.memset(ts_table[0:LAST, :], 0.0)
+        nc.scalar.activation(warm2[:], warm[:], ACT.Exp)
+        make_identity(nc, ident[:])
+        nc.gpsimd.memset(row_factors[0:LAST - 1, :], 0.0)
+
+        def turn_bank(name):
+            return psum.tile([P, 512], F32, name=name, tag="turn", bufs=3)
+
+        def turn_row(src, bank):
+            for j in range(TILES):
+                nc.tensor.transpose(bank[:, j * P:(j + 1) * P], src[:, j * P:(j + 1) * P], ident[:])
+
+        ts_neg_row = keep.tile([P, I], F32, name="ts_neg_row")
+        ts_pos_row = keep.tile([P, R], F32, name="ts_pos_row")
+        nc.vector.tensor_copy(ts_neg_row[:], ts_table[:].indirect(neg_list[:]))
+        nc.vector.tensor_copy(ts_pos_row[:], ts_table[:].indirect(pos_list[:]))
+
+        ts_neg = keep.tile([P, TILES], F32, name="ts_neg")
+        ts_pos = keep.tile([P, TILES], F32, name="ts_pos")
+        us_wt = keep.tile([P, 2, TILES], F32, name="us_wt")
+        bank = turn_bank("uw_bank")
+        turn_row(row_factors, bank)
+        nc.scalar.copy(us_wt[:], bank[:].rearrange("p (j q) -> p q j", q=P)[:, LAST - 1:P, :])
+        bank = turn_bank("tn_bank")
+        turn_row(ts_neg_row, bank)
+        nc.scalar.copy(ts_neg[:], bank[:, LAST::P])
+        bank = turn_bank("tp_bank")
+        turn_row(ts_pos_row, bank)
+        nc.scalar.copy(ts_pos[:], bank[:, LAST::P])
+        ts_neg_spread = psum.tile([P, I], F32, name="ts_neg_spread")
+        for j in range(TILES):
+            nc.tensor.transpose(ts_neg_spread[:, j * P:(j + 1) * P], ts_neg[:, j:j + 1].to_broadcast([P, P]), ident[:])
+
+        minus_us = keep.tile([P, TILES], F32, name="minus_us")
+        wt_us = keep.tile([P, TILES], F32, name="wt_us")
+        minus_us_tp = keep.tile([P, TILES], F32, name="minus_us_tp")
+        nc.scalar.mul(minus_us[:], us_wt[:, 0, :], -1.0)
+        nc.gpsimd.tensor_tensor(wt_us[:], us_wt[:, 0, :], us_wt[:, 1, :], ALU.mult)
+        nc.gpsimd.tensor_tensor(minus_us_tp[:], minus_us[:], ts_pos[:], ALU.mult)
+        wt_us_tp = keep.tile([P, TILES], F32, name="wt_us_tp")
+        nc.gpsimd.tensor_tensor(wt_us_tp[:], wt_us[:], ts_pos[:], ALU.mult)
+
+        w_neg = keep.tile([P, PACK, I], BF16, name="w_neg", align_bytes=64)
+        w_pos = [keep.tile([P, R], F32, name=f"w_pos{t}") for t in range(PACK)]
+        w_pos_rows = keep.tile([P, TILES, D], F32, name="w_pos_rows")
+        wd_grouped = keep.tile([P, I, PACK], BF16, name="wd_grouped", align_bytes=64)
+        wd_codes = keep.tile([P, I], U32, name="wd_codes", align_bytes=64)
+        wd_scales = keep.tile([P, I], U8, name="wd_scales", align_bytes=64)
+        x_bf = [keep.tile([P, D], BF16, name=f"x_bf{j}", align_bytes=64) for j in range(TILES)]
+        x_grouped = keep.tile([P, R, PACK], BF16, name="x_grouped", align_bytes=64)
+        x_codes = keep.tile([P, R], U32, name="x_codes", align_bytes=64)
+        x_scales = keep.tile([P, R], U8, name="x_scales", align_bytes=64)
+        wi_grouped = keep.tile([P, D, PACK], BF16, name="wi_grouped", align_bytes=64)
+        wi_codes = keep.tile([P, D], U32, name="wi_codes", align_bytes=64)
+        wi_scales = keep.tile([P, D], U8, name="wi_scales", align_bytes=64)
+
+        def gather_neg(t, first, count):
+            nc.vector.tensor_copy(
+                w_neg[:, t, first:first + count], planes[t][:].indirect(neg_list[:, first // 16:(first + count) // 16])
+            )
+
+        def gather_pos(t):
+            nc.vector.tensor_copy(w_pos[t][:], planes[t][:].indirect(pos_list[:]))
+            bank = turn_bank(f"pos_bank{t}")
+            turn_row(w_pos[t], bank)
+            nc.scalar.copy(
+                w_pos_rows[:].rearrange("r j (b t q) -> r t j b q", t=PACK, q=8)[:, t],
+                bank[:].rearrange("r (j b q) -> r j b q", j=TILES, q=8),
+            )
+
+        def group_wd(h):
+            cols = slice(h * HALF, (h + 1) * HALF)
+            nc.scalar.copy(
+                wd_grouped[:, cols, :].rearrange("p (c i) t -> p c t i", i=4),
+                w_neg[:, :, cols].rearrange("p t (c i) -> p c t i", i=4),
+            )
+            nc.vector.quantize_mx(
+                out=wd_codes[:, cols].bitcast(E4M3), scales=wd_scales[:, cols],
+                in_=wd_grouped[:, cols, :].rearrange("p i t -> p (i t)"),
+            )
+
+        def group_x(h):
+            bank = turn_bank(f"x_bank{h}")
+            for rr in range(2):
+                j = 2 * h + rr
+                nc.scalar.copy(
+                    x_bf[j][:].rearrange("r (u b q e) -> r u b q e", u=2, q=8, e=2),
+                    x_rows[j][:].rearrange("r (b u e q) -> r u b q e", u=2, q=8, e=2),
+                )
+                words = x_bf[j][:].bitcast(F32)
+                for u in range(2):
+                    nc.tensor.transpose(bank[:, (2 * rr + u) * P:(2 * rr + u + 1) * P], words[:, u * P:(u + 1) * P], ident[:])
+            rows = slice(h * HALF, (h + 1) * HALF)
+            nc.scalar.copy(
+                x_grouped[:, rows, :].rearrange("p r t -> p (r t)").bitcast(F32).rearrange("p (a r u) -> p a r u", a=2, u=2),
+                bank[:].rearrange("p (a u r) -> p a r u", a=2, u=2),
+            )
+            nc.vector.quantize_mx(
+                out=x_codes[:, rows].bitcast(E4M3), scales=x_scales[:, rows],
+                in_=x_grouped[:, rows, :].rearrange("p r t -> p (r t)"),
+            )
+
+        def turn_neg(m):
+            words = w_neg[:].rearrange("p t i -> p (t i)").bitcast(F32).rearrange("p (t w) -> p t w", t=PACK)
+            wi_words = wi_grouped[:].rearrange("s d k -> s (d k)").bitcast(F32).rearrange(
+                "s (b t q u) -> s t b q u", t=PACK, q=8, u=2)
+            bank = turn_bank(f"wi_bank{m}")
+            for a in range(2):
+                for u in range(2):
+                    nc.tensor.transpose(bank[:, (2 * a + u) * P:(2 * a + u + 1) * P], words[:, 2 * m + a, u::2], ident[:])
+            nc.scalar.copy(wi_words[:, 2 * m:2 * m + 2], bank[:].rearrange("s (a u b q) -> s a b q u", a=2, u=2, q=8))
+
+        scaled_T = [keep.tile([P, TILES, HALF], F32, name=f"scaled_T{h}") for h in range(2)]
+
+        def scores(h, jj):
+            rows = slice(h * HALF, (h + 1) * HALF)
+            acc = psum.tile([P, 2, HALF], F32, name="acc", tag="mx", bufs=2)
+            for a in range(2):
+                slots = slice((2 * jj + a) * P, (2 * jj + a + 1) * P)
+                nc.tensor.matmul_mx(
+                    out=acc[:, a, :], lhsT=wd_codes[:, slots].bitcast(E4M3), lhsT_scale=wd_scales[:, slots],
+                    rhs=x_codes[:, rows].bitcast(E4M3), rhs_scale=x_scales[:, rows], start=True, stop=True,
+                )
+            for a in range(2):
+                j = 2 * jj + a
+                nc.scalar.activation(scaled_T[h][:, j, :], acc[:, a, :], ACT.Copy, scale=ts_neg[:, j:j + 1])
+
+        products = [keep.tile([P, D], F32, name=f"products{j}") for j in range(TILES)]
+        minus_z = [keep.tile([P, I + 1], F32, name=f"minus_z{j}") for j in range(TILES)]
+        e = [keep.tile([P, I + 1], F32, name=f"e{j}") for j in range(TILES)]
+        g = [keep.tile([P, I], BF16, name=f"g{j}", align_bytes=64) for j in range(TILES)]
+        minus_m = keep.tile([P, TILES], F32, name="minus_m")
+        tot = keep.tile([P, TILES], F32, name="tot")
+        inv = keep.tile([P, TILES], F32, name="inv")
+        c = keep.tile([P, TILES], F32, name="c")
+        gp = keep.tile([P, TILES], F32, name="gp")
+        miss = keep.tile([P, TILES], F32, name="miss")
+
+        def positive_score(j):
+            nc.vector.scalar_tensor_tensor(
+                products[j][:], w_pos_rows[:, j, :], minus_us_tp[:, j:j + 1], x_rows[j][:], ALU.mult, ALU.mult,
+                accum_out=minus_z[j][:, I:I + 1],
+            )
+
+        def row_max(j):
+            h, rr = divmod(j, 2)
+            y = psum.tile([P, I], F32, name="y", tag="y", bufs=2)
+            for s in range(TILES):
+                nc.tensor.transpose(y[:, s * P:(s + 1) * P], scaled_T[h][:, s, rr * P:(rr + 1) * P], ident[:])
+            col = slice(j, j + 1)
+            nc.vector.tensor_scalar(
+                minus_z[j][:, 0:I], y[:], minus_us[:, col], minus_z[j][:, I:I + 1], ALU.mult, ALU.min, accum_out=minus_m[:, col]
+            )
+            nc.scalar.activation(e[j][:], minus_z[j][:], ACT.Exp, bias=minus_m[:, col], scale=-1.0, accum_out=tot[:, col])
+
+        g_grouped = [keep.tile([P, P, PACK], BF16, name=f"g_grouped{j}", align_bytes=64) for j in range(TILES)]
+        g_codes = [keep.tile([P, P], U32, name=f"g_codes{j}", align_bytes=64) for j in range(TILES)]
+        g_scales = [keep.tile([P, P], U8, name=f"g_scales{j}", align_bytes=64) for j in range(TILES)]
+
+        def factors(j):
+            col = slice(j, j + 1)
+            nc.vector.reciprocal(inv[:, col], tot[:, col])
+            nc.vector.tensor_tensor(c[:, col], inv[:, col], wt_us[:, col], ALU.mult)
+
+        def gradient(j):
+            col = slice(j, j + 1)
+            nc.vector.scalar_tensor_tensor(g[j][:], e[j][:, 0:I], c[:, col], ts_neg_spread[:], ALU.mult, ALU.mult)
+            bank = turn_bank(f"g_bank{j}")
+            words = g[j][:].bitcast(F32)
+            for u in range(2):
+                nc.tensor.transpose(bank[:, u * P:(u + 1) * P], words[:, u::2], ident[:])
+            nc.scalar.copy(
+                g_grouped[j][:].rearrange("p r t -> p (r t)").bitcast(F32).rearrange("p (r u) -> p r u", u=2),
+                bank[:, 0:2 * P].rearrange("p (u r) -> p r u", u=2),
+            )
+            nc.gpsimd.tensor_scalar(miss[:, col], e[j][:, I:I + 1], inv[:, col], -1.0, ALU.mult, ALU.add)
+            nc.gpsimd.tensor_tensor(gp[:, col], miss[:, col], wt_us_tp[:, col], ALU.mult)
+
+        result = [keep.tile([P, D], F32, name=f"result{j}") for j in range(TILES)]
+        gx = {}
+
+        def multiply(j):
+            nc.vector.quantize_mx(
+                out=g_codes[j][:].bitcast(E5M2), scales=g_scales[j][:], in_=g_grouped[j][:].rearrange("p r t -> p (r t)")
+            )
+            gx[j] = psum.tile([P, D], F32, name="gx", tag="mx", bufs=2)
+            nc.tensor.matmul_mx(
+                out=gx[j][:], lhsT=g_codes[j][:].bitcast(E5M2), lhsT_scale=g_scales[j][:],
+                rhs=wi_codes[:].bitcast(E4M3), rhs_scale=wi_scales[:], start=True, stop=True,
+            )
+
+        def finish(j):
+            nc.vector.scalar_tensor_tensor(result[j][:], w_pos_rows[:, j, :], gp[:, j:j + 1], gx[j][:], ALU.mult, ALU.add)
+            nc.sync.dma_start(out[j * P:(j + 1) * P, :], result[j][:])
+
+        gather_neg(0, 0, I)
+        gather_pos(0)
+        group_x(0)
+        gather_neg(1, 0, I)
+        gather_pos(1)
+        turn_neg(0)
+        gather_neg(2, 0, I)
+        gather_pos(2)
+        group_x(1)
+        gather_neg(3, 0, HALF)
+        gather_neg(3, HALF, HALF)
+        group_wd(0)
+        gather_pos(3)
+        group_wd(1)
+        scores(0, 0)
+        scores(0, 1)
+        for j in range(TILES):
+            positive_score(j)
+        row_max(0)
+        scores(1, 0)
+        scores(1, 1)
+        row_max(1)
+        turn_neg(1)
+        row_max(2)
+        factors(0)
+        row_max(3)
+        nc.vector.quantize_mx(
+            out=wi_codes[:].bitcast(E4M3), scales=wi_scales[:], in_=wi_grouped[:].rearrange("s d k -> s (d k)")
+        )
+        gradient(0)
+        factors(1)
+        gradient(1)
+        factors(2)
+        gradient(2)
+        factors(3)
+        multiply(0)
+        gradient(3)
+        multiply(1)
+        finish(0)
+        multiply(2)
+        finish(1)
+        multiply(3)
+        finish(2)
+        finish(3)

@@ -21,7 +21,7 @@ PACK = 4
 TILES = 4
 HALF = 256
 LAST = P - 1
-ORDER = [("w", 0), ("x", 0), ("x", 1), ("w", 1), ("x", 2), ("w", 2), ("x", 3), ("w", 3)]
+ORDER = [("w", 0), ("w", 1), ("x", 0), ("x", 1), ("w", 2), ("w", 3), ("x", 2), ("x", 3)]
 
 
 def tile_attend_gspos_sm_x_kernel(tc, x, wT, us, ts, wt, offs, poffs, out):
@@ -40,7 +40,7 @@ def tile_attend_gspos_sm_x_kernel(tc, x, wT, us, ts, wt, offs, poffs, out):
         warm = keep.tile([P, 1], F32, name="warm")
         warm2 = keep.tile([P, 1], F32, name="warm2")
 
-        wT_planes = wT.rearrange("(b t q) c -> t b q c", t=PACK, q=8)
+        wT_planes = wT.rearrange("(p t) c -> t p c", t=PACK)
         nc.sync.dma_start(neg_list[:], offs)
         nc.sync.dma_start(ts_table[LAST:P, :], ts[0:1, :])
         nc.sync.dma_start(pos_list[:], poffs)
@@ -59,7 +59,7 @@ def tile_attend_gspos_sm_x_kernel(tc, x, wT, us, ts, wt, offs, poffs, out):
         nc.gpsimd.memset(row_factors[0:LAST - 1, :], 0.0)
 
         def turn_bank(name):
-            return psum.tile([P, 512], F32, name=name, tag="turn", bufs=3)
+            return psum.tile([P, 512], F32, name=name, tag="turn", bufs=4)
 
         def turn_row(src, bank):
             for j in range(TILES):
@@ -71,33 +71,35 @@ def tile_attend_gspos_sm_x_kernel(tc, x, wT, us, ts, wt, offs, poffs, out):
         nc.vector.tensor_copy(ts_pos_row[:], ts_table[:].indirect(pos_list[:]))
 
         ts_neg = keep.tile([P, TILES], F32, name="ts_neg")
-        ts_pos = keep.tile([P, TILES], F32, name="ts_pos")
-        us_wt = keep.tile([P, 2, TILES], F32, name="us_wt")
+        ts_neg_spread = keep.tile([P, I], F32, name="ts_neg_spread")
+        us_col = keep.tile([P, TILES], F32, name="us_col")
+        minus_us = keep.tile([P, TILES], F32, name="minus_us")
+        wt_us = keep.tile([P, TILES], F32, name="wt_us")
+        minus_us_tp = keep.tile([P, TILES], F32, name="minus_us_tp")
+        wt_us_tp = keep.tile([P, TILES], F32, name="wt_us_tp")
         bank = turn_bank("uw_bank")
         turn_row(row_factors, bank)
-        nc.scalar.copy(us_wt[:], bank[:].rearrange("p (j q) -> p q j", q=P)[:, LAST - 1:P, :])
+        nc.scalar.copy(us_col[:], bank[:, LAST - 1::P])
+        nc.scalar.mul(minus_us[:], bank[:, LAST - 1::P], -1.0)
+        for j in range(TILES):
+            nc.scalar.mul(wt_us[:, j:j + 1], bank[:, j * P + LAST:(j + 1) * P], us_col[:, j:j + 1])
         bank = turn_bank("tn_bank")
         turn_row(ts_neg_row, bank)
         nc.scalar.copy(ts_neg[:], bank[:, LAST::P])
         bank = turn_bank("tp_bank")
         turn_row(ts_pos_row, bank)
-        nc.scalar.copy(ts_pos[:], bank[:, LAST::P])
-        ts_neg_spread = psum.tile([P, I], F32, name="ts_neg_spread")
         for j in range(TILES):
-            nc.tensor.transpose(ts_neg_spread[:, j * P:(j + 1) * P], ts_neg[:, j:j + 1].to_broadcast([P, P]), ident[:])
-
-        minus_us = keep.tile([P, TILES], F32, name="minus_us")
-        wt_us = keep.tile([P, TILES], F32, name="wt_us")
-        minus_us_tp = keep.tile([P, TILES], F32, name="minus_us_tp")
-        nc.scalar.mul(minus_us[:], us_wt[:, 0, :], -1.0)
-        nc.gpsimd.tensor_tensor(wt_us[:], us_wt[:, 0, :], us_wt[:, 1, :], ALU.mult)
-        nc.gpsimd.tensor_tensor(minus_us_tp[:], minus_us[:], ts_pos[:], ALU.mult)
-        wt_us_tp = keep.tile([P, TILES], F32, name="wt_us_tp")
-        nc.gpsimd.tensor_tensor(wt_us_tp[:], wt_us[:], ts_pos[:], ALU.mult)
+            ts_pos = bank[:, j * P + LAST:(j + 1) * P]
+            nc.scalar.mul(minus_us_tp[:, j:j + 1], ts_pos, minus_us[:, j:j + 1])
+            nc.scalar.mul(wt_us_tp[:, j:j + 1], ts_pos, wt_us[:, j:j + 1])
+        bank = turn_bank("spread_bank")
+        for j in range(TILES):
+            nc.tensor.transpose(bank[:, j * P:(j + 1) * P], ts_neg[:, j:j + 1].to_broadcast([P, P]), ident[:])
+        nc.scalar.copy(ts_neg_spread[:], bank[:])
 
         w_neg = keep.tile([P, PACK, I], BF16, name="w_neg", align_bytes=64)
         w_pos = [keep.tile([P, R], F32, name=f"w_pos{t}") for t in range(PACK)]
-        w_pos_rows = keep.tile([P, TILES, D], F32, name="w_pos_rows")
+        w_pos_rows = [keep.tile([P, D], F32, name=f"w_pos_rows{j}") for j in range(TILES)]
         wd_grouped = keep.tile([P, I, PACK], BF16, name="wd_grouped", align_bytes=64)
         wd_codes = keep.tile([P, I], U32, name="wd_codes", align_bytes=64)
         wd_scales = keep.tile([P, I], U8, name="wd_scales", align_bytes=64)
@@ -116,12 +118,6 @@ def tile_attend_gspos_sm_x_kernel(tc, x, wT, us, ts, wt, offs, poffs, out):
 
         def gather_pos(t):
             nc.vector.tensor_copy(w_pos[t][:], planes[t][:].indirect(pos_list[:]))
-            bank = turn_bank(f"pos_bank{t}")
-            turn_row(w_pos[t], bank)
-            nc.scalar.copy(
-                w_pos_rows[:].rearrange("r j (b t q) -> r t j b q", t=PACK, q=8)[:, t],
-                bank[:].rearrange("r (j b q) -> r j b q", j=TILES, q=8),
-            )
 
         def group_wd(h):
             cols = slice(h * HALF, (h + 1) * HALF)
@@ -139,8 +135,8 @@ def tile_attend_gspos_sm_x_kernel(tc, x, wT, us, ts, wt, offs, poffs, out):
             for rr in range(2):
                 j = 2 * h + rr
                 nc.scalar.copy(
-                    x_bf[j][:].rearrange("r (u b q e) -> r u b q e", u=2, q=8, e=2),
-                    x_rows[j][:].rearrange("r (b u e q) -> r u b q e", u=2, q=8, e=2),
+                    x_bf[j][:].rearrange("r (u p e) -> r u p e", u=2, e=2),
+                    x_rows[j][:].rearrange("r (p u e) -> r u p e", u=2, e=2),
                 )
                 words = x_bf[j][:].bitcast(F32)
                 for u in range(2):
@@ -158,12 +154,12 @@ def tile_attend_gspos_sm_x_kernel(tc, x, wT, us, ts, wt, offs, poffs, out):
         def turn_neg(m):
             words = w_neg[:].rearrange("p t i -> p (t i)").bitcast(F32).rearrange("p (t w) -> p t w", t=PACK)
             wi_words = wi_grouped[:].rearrange("s d k -> s (d k)").bitcast(F32).rearrange(
-                "s (b t q u) -> s t b q u", t=PACK, q=8, u=2)
+                "s (p t u) -> s p t u", t=PACK, u=2)
             bank = turn_bank(f"wi_bank{m}")
-            for a in range(2):
+            for a in reversed(range(2)):
                 for u in range(2):
                     nc.tensor.transpose(bank[:, (2 * a + u) * P:(2 * a + u + 1) * P], words[:, 2 * m + a, u::2], ident[:])
-            nc.scalar.copy(wi_words[:, 2 * m:2 * m + 2], bank[:].rearrange("s (a u b q) -> s a b q u", a=2, u=2, q=8))
+            nc.scalar.copy(wi_words[:, :, 2 * m:2 * m + 2, :], bank[:].rearrange("s (a u p) -> s p a u", a=2, u=2))
 
         scaled_T = [keep.tile([P, TILES, HALF], F32, name=f"scaled_T{h}") for h in range(2)]
 
@@ -182,7 +178,7 @@ def tile_attend_gspos_sm_x_kernel(tc, x, wT, us, ts, wt, offs, poffs, out):
 
         products = [keep.tile([P, D], F32, name=f"products{j}") for j in range(TILES)]
         minus_z = [keep.tile([P, I + 1], F32, name=f"minus_z{j}") for j in range(TILES)]
-        e = [keep.tile([P, I + 1], F32, name=f"e{j}") for j in range(TILES)]
+        e = keep.tile([P, TILES, I + 8], F32, name="e")
         g = [keep.tile([P, I], BF16, name=f"g{j}", align_bytes=64) for j in range(TILES)]
         minus_m = keep.tile([P, TILES], F32, name="minus_m")
         tot = keep.tile([P, TILES], F32, name="tot")
@@ -191,11 +187,21 @@ def tile_attend_gspos_sm_x_kernel(tc, x, wT, us, ts, wt, offs, poffs, out):
         gp = keep.tile([P, TILES], F32, name="gp")
         miss = keep.tile([P, TILES], F32, name="miss")
 
+        pos_banks = {}
+
         def positive_score(j):
+            bank = turn_bank(f"pos_bank{j}")
+            for t in reversed(range(PACK)):
+                nc.tensor.transpose(bank[:, t * P:(t + 1) * P], w_pos[t][:, j * P:(j + 1) * P], ident[:])
+            pos_banks[j] = bank[:].rearrange("r (t p) -> r p t", t=PACK)
             nc.vector.scalar_tensor_tensor(
-                products[j][:], w_pos_rows[:, j, :], minus_us_tp[:, j:j + 1], x_rows[j][:], ALU.mult, ALU.mult,
+                products[j][:].rearrange("r (p t) -> r p t", t=PACK), pos_banks[j], minus_us_tp[:, j:j + 1],
+                x_rows[j][:].rearrange("r (p t) -> r p t", t=PACK), ALU.mult, ALU.mult,
                 accum_out=minus_z[j][:, I:I + 1],
             )
+
+        def keep_positives(j):
+            nc.scalar.copy(w_pos_rows[j][:].rearrange("r (p t) -> r p t", t=PACK), pos_banks[j])
 
         def row_max(j):
             h, rr = divmod(j, 2)
@@ -206,7 +212,7 @@ def tile_attend_gspos_sm_x_kernel(tc, x, wT, us, ts, wt, offs, poffs, out):
             nc.vector.tensor_scalar(
                 minus_z[j][:, 0:I], y[:], minus_us[:, col], minus_z[j][:, I:I + 1], ALU.mult, ALU.min, accum_out=minus_m[:, col]
             )
-            nc.scalar.activation(e[j][:], minus_z[j][:], ACT.Exp, bias=minus_m[:, col], scale=-1.0, accum_out=tot[:, col])
+            nc.scalar.activation(e[:, j, 0:I + 1], minus_z[j][:], ACT.Exp, bias=minus_m[:, col], scale=-1.0, accum_out=tot[:, col])
 
         g_grouped = [keep.tile([P, P, PACK], BF16, name=f"g_grouped{j}", align_bytes=64) for j in range(TILES)]
         g_codes = [keep.tile([P, P], U32, name=f"g_codes{j}", align_bytes=64) for j in range(TILES)]
@@ -219,8 +225,8 @@ def tile_attend_gspos_sm_x_kernel(tc, x, wT, us, ts, wt, offs, poffs, out):
 
         def gradient(j):
             col = slice(j, j + 1)
-            nc.vector.scalar_tensor_tensor(g[j][:], e[j][:, 0:I], c[:, col], ts_neg_spread[:], ALU.mult, ALU.mult)
-            bank = turn_bank(f"g_bank{j}")
+            nc.vector.scalar_tensor_tensor(g[j][:], e[:, j, 0:I], c[:, col], ts_neg_spread[:], ALU.mult, ALU.mult)
+            bank = psum.tile([P, 512], F32, name=f"g_bank{j}", tag="y", bufs=2)
             words = g[j][:].bitcast(F32)
             for u in range(2):
                 nc.tensor.transpose(bank[:, u * P:(u + 1) * P], words[:, u::2], ident[:])
@@ -228,8 +234,6 @@ def tile_attend_gspos_sm_x_kernel(tc, x, wT, us, ts, wt, offs, poffs, out):
                 g_grouped[j][:].rearrange("p r t -> p (r t)").bitcast(F32).rearrange("p (r u) -> p r u", u=2),
                 bank[:, 0:2 * P].rearrange("p (u r) -> p r u", u=2),
             )
-            nc.gpsimd.tensor_scalar(miss[:, col], e[j][:, I:I + 1], inv[:, col], -1.0, ALU.mult, ALU.add)
-            nc.gpsimd.tensor_tensor(gp[:, col], miss[:, col], wt_us_tp[:, col], ALU.mult)
 
         result = [keep.tile([P, D], F32, name=f"result{j}") for j in range(TILES)]
         gx = {}
@@ -245,7 +249,7 @@ def tile_attend_gspos_sm_x_kernel(tc, x, wT, us, ts, wt, offs, poffs, out):
             )
 
         def finish(j):
-            nc.vector.scalar_tensor_tensor(result[j][:], w_pos_rows[:, j, :], gp[:, j:j + 1], gx[j][:], ALU.mult, ALU.add)
+            nc.vector.scalar_tensor_tensor(result[j][:], w_pos_rows[j][:], gp[:, j:j + 1], gx[j][:], ALU.mult, ALU.add)
             nc.sync.dma_start(out[j * P:(j + 1) * P, :], result[j][:])
 
         gather_neg(0, 0, I)
@@ -255,8 +259,8 @@ def tile_attend_gspos_sm_x_kernel(tc, x, wT, us, ts, wt, offs, poffs, out):
         gather_pos(1)
         turn_neg(0)
         gather_neg(2, 0, I)
-        gather_pos(2)
         group_x(1)
+        gather_pos(2)
         gather_neg(3, 0, HALF)
         gather_neg(3, HALF, HALF)
         group_wd(0)
@@ -270,6 +274,7 @@ def tile_attend_gspos_sm_x_kernel(tc, x, wT, us, ts, wt, offs, poffs, out):
         scores(1, 0)
         scores(1, 1)
         row_max(1)
+        keep_positives(0)
         turn_neg(1)
         row_max(2)
         factors(0)
@@ -285,7 +290,12 @@ def tile_attend_gspos_sm_x_kernel(tc, x, wT, us, ts, wt, offs, poffs, out):
         factors(3)
         multiply(0)
         gradient(3)
+        nc.vector.tensor_tensor(miss[:], e[:, :, I], inv[:], ALU.mult)
         multiply(1)
+        nc.vector.scalar_tensor_tensor(gp[:], miss[:], -1.0, wt_us_tp[:], ALU.add, ALU.mult)
+        keep_positives(1)
+        keep_positives(2)
+        keep_positives(3)
         finish(0)
         multiply(2)
         finish(1)

@@ -21,7 +21,10 @@ PACK = 4
 TILES = 4
 HALF = 256
 LAST = P - 1
-ORDER = [("w", 0), ("w", 1), ("x", 0), ("x", 1), ("w", 2), ("w", 3), ("x", 2), ("x", 3)]
+PTAG = "products"
+LATE = ["late0", "late1"]
+PROD = ["wd1", "wd0", "p2", "p3"]
+ORDER = [("w", 0), ("w", 1), ("x", 0), ("x", 1), ("w", 2), ("x", 2), ("w", 3), ("x", 3)]
 
 
 def tile_attend_gspos_sm_x_kernel(tc, x, wT, us, ts, wt, offs, poffs, out):
@@ -42,13 +45,13 @@ def tile_attend_gspos_sm_x_kernel(tc, x, wT, us, ts, wt, offs, poffs, out):
 
         wT_planes = wT.rearrange("(p t) c -> t p c", t=PACK)
         nc.sync.dma_start(neg_list[:], offs)
-        nc.sync.dma_start(ts_table[LAST:P, :], ts[0:1, :])
         nc.sync.dma_start(pos_list[:], poffs)
         for kind, n in ORDER:
             if kind == "w":
                 nc.sync.dma_start(planes[n][:], wT_planes[n])
             else:
                 nc.sync.dma_start(x_rows[n][:], x[n * P:(n + 1) * P, :])
+        nc.scalar.dma_start(ts_table[LAST:P, :], ts[0:1, :])
         nc.scalar.dma_start(row_factors[LAST - 1:LAST, :], us.rearrange("r o -> o r"))
         nc.scalar.dma_start(row_factors[LAST:P, :], wt.rearrange("r o -> o r"))
 
@@ -58,8 +61,8 @@ def tile_attend_gspos_sm_x_kernel(tc, x, wT, us, ts, wt, offs, poffs, out):
         make_identity(nc, ident[:])
         nc.gpsimd.memset(row_factors[0:LAST - 1, :], 0.0)
 
-        def turn_bank(name):
-            return psum.tile([P, 512], F32, name=name, tag="turn", bufs=4)
+        def turn_bank(name, tag):
+            return psum.tile([P, 512], F32, name=name, tag=tag)
 
         def turn_row(src, bank):
             for j in range(TILES):
@@ -71,44 +74,40 @@ def tile_attend_gspos_sm_x_kernel(tc, x, wT, us, ts, wt, offs, poffs, out):
         nc.vector.tensor_copy(ts_pos_row[:], ts_table[:].indirect(pos_list[:]))
 
         ts_neg = keep.tile([P, TILES], F32, name="ts_neg")
-        ts_neg_spread = keep.tile([P, I], F32, name="ts_neg_spread")
+        ts_neg_spread = keep.tile([P, I], F32, name="ts_neg_spread", tag="spread", align_bytes=64)
         us_col = keep.tile([P, TILES], F32, name="us_col")
         minus_us = keep.tile([P, TILES], F32, name="minus_us")
         wt_us = keep.tile([P, TILES], F32, name="wt_us")
         minus_us_tp = keep.tile([P, TILES], F32, name="minus_us_tp")
         wt_us_tp = keep.tile([P, TILES], F32, name="wt_us_tp")
-        bank = turn_bank("uw_bank")
+        bank = turn_bank("uw_bank", "b0")
         turn_row(row_factors, bank)
         nc.scalar.copy(us_col[:], bank[:, LAST - 1::P])
         nc.scalar.mul(minus_us[:], bank[:, LAST - 1::P], -1.0)
         for j in range(TILES):
             nc.scalar.mul(wt_us[:, j:j + 1], bank[:, j * P + LAST:(j + 1) * P], us_col[:, j:j + 1])
-        bank = turn_bank("tn_bank")
+        bank = turn_bank("tn_bank", "b1")
         turn_row(ts_neg_row, bank)
         nc.scalar.copy(ts_neg[:], bank[:, LAST::P])
-        bank = turn_bank("tp_bank")
+        bank = turn_bank("tp_bank", "b2")
         turn_row(ts_pos_row, bank)
         for j in range(TILES):
             ts_pos = bank[:, j * P + LAST:(j + 1) * P]
             nc.scalar.mul(minus_us_tp[:, j:j + 1], ts_pos, minus_us[:, j:j + 1])
             nc.scalar.mul(wt_us_tp[:, j:j + 1], ts_pos, wt_us[:, j:j + 1])
-        bank = turn_bank("spread_bank")
+        bank = turn_bank("spread_bank", "b3")
         for j in range(TILES):
             nc.tensor.transpose(bank[:, j * P:(j + 1) * P], ts_neg[:, j:j + 1].to_broadcast([P, P]), ident[:])
         nc.scalar.copy(ts_neg_spread[:], bank[:])
 
         w_neg = keep.tile([P, PACK, I], BF16, name="w_neg", align_bytes=64)
         w_pos = [keep.tile([P, R], F32, name=f"w_pos{t}") for t in range(PACK)]
-        w_pos_rows = [keep.tile([P, D], F32, name=f"w_pos_rows{j}") for j in range(TILES)]
-        wd_grouped = keep.tile([P, I, PACK], BF16, name="wd_grouped", align_bytes=64)
         wd_codes = keep.tile([P, I], U32, name="wd_codes", align_bytes=64)
         wd_scales = keep.tile([P, I], U8, name="wd_scales", align_bytes=64)
         x_bf = [keep.tile([P, D], BF16, name=f"x_bf{j}", align_bytes=64) for j in range(TILES)]
-        x_grouped = keep.tile([P, R, PACK], BF16, name="x_grouped", align_bytes=64)
         x_codes = keep.tile([P, R], U32, name="x_codes", align_bytes=64)
         x_scales = keep.tile([P, R], U8, name="x_scales", align_bytes=64)
         wi_grouped = keep.tile([P, D, PACK], BF16, name="wi_grouped", align_bytes=64)
-        wi_codes = keep.tile([P, D], U32, name="wi_codes", align_bytes=64)
         wi_scales = keep.tile([P, D], U8, name="wi_scales", align_bytes=64)
 
         def gather_neg(t, first, count):
@@ -121,51 +120,55 @@ def tile_attend_gspos_sm_x_kernel(tc, x, wT, us, ts, wt, offs, poffs, out):
 
         def group_wd(h):
             cols = slice(h * HALF, (h + 1) * HALF)
+            wd_grouped = keep.tile([P, HALF, PACK], BF16, name="wd_grouped", tag=f"wd{h}", align_bytes=64)
             nc.scalar.copy(
-                wd_grouped[:, cols, :].rearrange("p (c i) t -> p c t i", i=4),
+                wd_grouped[:].rearrange("p (c i) t -> p c t i", i=4),
                 w_neg[:, :, cols].rearrange("p t (c i) -> p c t i", i=4),
             )
             nc.vector.quantize_mx(
                 out=wd_codes[:, cols].bitcast(E4M3), scales=wd_scales[:, cols],
-                in_=wd_grouped[:, cols, :].rearrange("p i t -> p (i t)"),
+                in_=wd_grouped[:].rearrange("p i t -> p (i t)"),
             )
 
-        def group_x(h):
-            bank = turn_bank(f"x_bank{h}")
-            for rr in range(2):
-                j = 2 * h + rr
-                nc.scalar.copy(
-                    x_bf[j][:].rearrange("r (u p e) -> r u p e", u=2, e=2),
-                    x_rows[j][:].rearrange("r (p u e) -> r u p e", u=2, e=2),
-                )
+        def cast_x(j):
+            nc.scalar.copy(
+                x_bf[j][:].rearrange("r (u p e) -> r u p e", u=2, e=2),
+                x_rows[j][:].rearrange("r (p u e) -> r u p e", u=2, e=2),
+            )
+
+        def group_x(tiles, tag):
+            bank = psum.tile([P, 512], F32, name="x_bank", tag=tag)
+            n = len(tiles)
+            for rr, j in enumerate(tiles):
                 words = x_bf[j][:].bitcast(F32)
                 for u in range(2):
                     nc.tensor.transpose(bank[:, (2 * rr + u) * P:(2 * rr + u + 1) * P], words[:, u * P:(u + 1) * P], ident[:])
-            rows = slice(h * HALF, (h + 1) * HALF)
+            rows = slice(tiles[0] * P, (tiles[0] + n) * P)
+            x_grouped = keep.tile([P, n * P, PACK], BF16, name="x_grouped", tag=f"xg{tiles[0]}", align_bytes=64)
             nc.scalar.copy(
-                x_grouped[:, rows, :].rearrange("p r t -> p (r t)").bitcast(F32).rearrange("p (a r u) -> p a r u", a=2, u=2),
-                bank[:].rearrange("p (a u r) -> p a r u", a=2, u=2),
+                x_grouped[:].rearrange("p r t -> p (r t)").bitcast(F32).rearrange("p (a r u) -> p a r u", a=n, u=2),
+                bank[:, 0:n * HALF].rearrange("p (a u r) -> p a r u", a=n, u=2),
             )
             nc.vector.quantize_mx(
                 out=x_codes[:, rows].bitcast(E4M3), scales=x_scales[:, rows],
-                in_=x_grouped[:, rows, :].rearrange("p r t -> p (r t)"),
+                in_=x_grouped[:].rearrange("p r t -> p (r t)"),
             )
 
-        def turn_neg(m):
+        def turn_neg(m, tag):
             words = w_neg[:].rearrange("p t i -> p (t i)").bitcast(F32).rearrange("p (t w) -> p t w", t=PACK)
             wi_words = wi_grouped[:].rearrange("s d k -> s (d k)").bitcast(F32).rearrange(
                 "s (p t u) -> s p t u", t=PACK, u=2)
-            bank = turn_bank(f"wi_bank{m}")
+            bank = psum.tile([P, 512], F32, name="wi_bank", tag=tag)
             for a in reversed(range(2)):
                 for u in range(2):
                     nc.tensor.transpose(bank[:, (2 * a + u) * P:(2 * a + u + 1) * P], words[:, 2 * m + a, u::2], ident[:])
             nc.scalar.copy(wi_words[:, :, 2 * m:2 * m + 2, :], bank[:].rearrange("s (a u p) -> s p a u", a=2, u=2))
 
-        scaled_T = [keep.tile([P, TILES, HALF], F32, name=f"scaled_T{h}") for h in range(2)]
+        scaled_T = [keep.tile([P, TILES, HALF], F32, name=f"scaled_T{h}", tag=f"late{h}") for h in range(2)]
 
-        def scores(h, jj):
+        def scores(h, jj, tag):
             rows = slice(h * HALF, (h + 1) * HALF)
-            acc = psum.tile([P, 2, HALF], F32, name="acc", tag="mx", bufs=2)
+            acc = psum.tile([P, 2, HALF], F32, name="acc", tag=tag)
             for a in range(2):
                 slots = slice((2 * jj + a) * P, (2 * jj + a + 1) * P)
                 nc.tensor.matmul_mx(
@@ -176,8 +179,7 @@ def tile_attend_gspos_sm_x_kernel(tc, x, wT, us, ts, wt, offs, poffs, out):
                 j = 2 * jj + a
                 nc.scalar.activation(scaled_T[h][:, j, :], acc[:, a, :], ACT.Copy, scale=ts_neg[:, j:j + 1])
 
-        products = [keep.tile([P, D], F32, name=f"products{j}") for j in range(TILES)]
-        minus_z = [keep.tile([P, I + 1], F32, name=f"minus_z{j}") for j in range(TILES)]
+        minus_z = [keep.tile([P, I + 1], F32, name=f"minus_z{j}", tag=f"minus_z{j}") for j in range(TILES)]
         e = keep.tile([P, TILES, I + 8], F32, name="e")
         g = [keep.tile([P, I], BF16, name=f"g{j}", align_bytes=64) for j in range(TILES)]
         minus_m = keep.tile([P, TILES], F32, name="minus_m")
@@ -188,24 +190,47 @@ def tile_attend_gspos_sm_x_kernel(tc, x, wT, us, ts, wt, offs, poffs, out):
         miss = keep.tile([P, TILES], F32, name="miss")
 
         pos_banks = {}
+        junk = {}
 
-        def positive_score(j):
-            bank = turn_bank(f"pos_bank{j}")
-            for t in reversed(range(PACK)):
+        def positive_score(j, tag, n):
+            bank = turn_bank(f"pos_bank{j}", f"b{4 + j}")
+            for t in (2, 0, 1, 3):
                 nc.tensor.transpose(bank[:, t * P:(t + 1) * P], w_pos[t][:, j * P:(j + 1) * P], ident[:])
             pos_banks[j] = bank[:].rearrange("r (t p) -> r p t", t=PACK)
+            if tag not in junk:
+                junk[tag] = keep.tile([P, 2, D], F32, name="products", tag=tag, align_bytes=64)
+            products = junk[tag][:, n, :]
             nc.vector.scalar_tensor_tensor(
-                products[j][:].rearrange("r (p t) -> r p t", t=PACK), pos_banks[j], minus_us_tp[:, j:j + 1],
+                products.rearrange("r (p t) -> r p t", t=PACK), pos_banks[j], minus_us_tp[:, j:j + 1],
                 x_rows[j][:].rearrange("r (p t) -> r p t", t=PACK), ALU.mult, ALU.mult,
                 accum_out=minus_z[j][:, I:I + 1],
             )
 
-        def keep_positives(j):
-            nc.scalar.copy(w_pos_rows[j][:].rearrange("r (p t) -> r p t", t=PACK), pos_banks[j])
+        w_pos_rows = {}
 
-        def row_max(j):
+        def keep_positives(tiles, tag):
+            kept = keep.tile([P, len(tiles), D], F32, name="w_pos_rows", tag=tag)
+            for n, j in enumerate(tiles):
+                w_pos_rows[j] = kept[:, n, :]
+                nc.scalar.copy(w_pos_rows[j].rearrange("r (p t) -> r p t", t=PACK), pos_banks[j])
+
+        def direct_scores(j, tag):
+            rows = slice(j * P, (j + 1) * P)
+            acc = psum.tile([P, I], F32, name="a", tag=tag)
+            nc.tensor.matmul_mx(
+                out=acc[:], lhsT=x_codes[:, rows].bitcast(E4M3), lhsT_scale=x_scales[:, rows],
+                rhs=wd_codes[:].bitcast(E4M3), rhs_scale=wd_scales[:], start=True, stop=True,
+            )
+            nc.vector.scalar_tensor_tensor(minus_z[j][:, 0:I], acc[:], minus_us[:, j:j + 1], ts_neg_spread[:], ALU.mult, ALU.mult)
+
+        def direct_max(j):
+            col = slice(j, j + 1)
+            nc.vector.tensor_reduce(minus_m[:, col], minus_z[j][:], mybir.AxisListType.X, ALU.min)
+            nc.scalar.activation(e[:, j, 0:I + 1], minus_z[j][:], ACT.Exp, bias=minus_m[:, col], scale=-1.0, accum_out=tot[:, col])
+
+        def row_max(j, tag):
             h, rr = divmod(j, 2)
-            y = psum.tile([P, I], F32, name="y", tag="y", bufs=2)
+            y = psum.tile([P, I], F32, name="y", tag=tag)
             for s in range(TILES):
                 nc.tensor.transpose(y[:, s * P:(s + 1) * P], scaled_T[h][:, s, rr * P:(rr + 1) * P], ident[:])
             col = slice(j, j + 1)
@@ -221,12 +246,12 @@ def tile_attend_gspos_sm_x_kernel(tc, x, wT, us, ts, wt, offs, poffs, out):
         def factors(j):
             col = slice(j, j + 1)
             nc.vector.reciprocal(inv[:, col], tot[:, col])
-            nc.vector.tensor_tensor(c[:, col], inv[:, col], wt_us[:, col], ALU.mult)
+            nc.scalar.mul(c[:, col], inv[:, col], wt_us[:, col])
 
-        def gradient(j):
+        def gradient(j, tag):
             col = slice(j, j + 1)
             nc.vector.scalar_tensor_tensor(g[j][:], e[:, j, 0:I], c[:, col], ts_neg_spread[:], ALU.mult, ALU.mult)
-            bank = psum.tile([P, 512], F32, name=f"g_bank{j}", tag="y", bufs=2)
+            bank = psum.tile([P, 512], F32, name=f"g_bank{j}", tag=tag)
             words = g[j][:].bitcast(F32)
             for u in range(2):
                 nc.tensor.transpose(bank[:, u * P:(u + 1) * P], words[:, u::2], ident[:])
@@ -235,70 +260,81 @@ def tile_attend_gspos_sm_x_kernel(tc, x, wT, us, ts, wt, offs, poffs, out):
                 bank[:, 0:2 * P].rearrange("p (u r) -> p r u", u=2),
             )
 
+        wi = {}
+
+        def quantise_wi(tag):
+            wi[0] = keep.tile([P, D], U32, name="wi_codes", tag=tag, align_bytes=64)
+            nc.vector.quantize_mx(out=wi[0][:].bitcast(E4M3), scales=wi_scales[:], in_=wi_grouped[:].rearrange("s d k -> s (d k)"))
+
         result = [keep.tile([P, D], F32, name=f"result{j}") for j in range(TILES)]
         gx = {}
 
-        def multiply(j):
+        def multiply(j, tag):
             nc.vector.quantize_mx(
                 out=g_codes[j][:].bitcast(E5M2), scales=g_scales[j][:], in_=g_grouped[j][:].rearrange("p r t -> p (r t)")
             )
-            gx[j] = psum.tile([P, D], F32, name="gx", tag="mx", bufs=2)
+            gx[j] = psum.tile([P, D], F32, name="gx", tag=tag)
             nc.tensor.matmul_mx(
                 out=gx[j][:], lhsT=g_codes[j][:].bitcast(E5M2), lhsT_scale=g_scales[j][:],
-                rhs=wi_codes[:].bitcast(E4M3), rhs_scale=wi_scales[:], start=True, stop=True,
+                rhs=wi[0][:].bitcast(E4M3), rhs_scale=wi_scales[:], start=True, stop=True,
             )
 
-        def finish(j):
-            nc.vector.scalar_tensor_tensor(result[j][:], w_pos_rows[j][:], gp[:, j:j + 1], gx[j][:], ALU.mult, ALU.add)
-            nc.sync.dma_start(out[j * P:(j + 1) * P, :], result[j][:])
+        def finish(j, pieces=1):
+            width = D // pieces
+            for n in range(pieces):
+                cols = slice(n * width, (n + 1) * width)
+                nc.vector.scalar_tensor_tensor(result[j][:, cols], w_pos_rows[j][:, cols], gp[:, j:j + 1], gx[j][:, cols], ALU.mult, ALU.add)
+                nc.sync.dma_start(out[j * P:(j + 1) * P, cols], result[j][:, cols])
 
         gather_neg(0, 0, I)
         gather_pos(0)
-        group_x(0)
         gather_neg(1, 0, I)
         gather_pos(1)
-        turn_neg(0)
+        turn_neg(0,"b0")
         gather_neg(2, 0, I)
-        group_x(1)
         gather_pos(2)
         gather_neg(3, 0, HALF)
         gather_neg(3, HALF, HALF)
+        cast_x(0)
+        cast_x(1)
+        group_x([0,1],"b1")
         group_wd(0)
-        gather_pos(3)
         group_wd(1)
-        scores(0, 0)
-        scores(0, 1)
-        for j in range(TILES):
-            positive_score(j)
-        row_max(0)
-        scores(1, 0)
-        scores(1, 1)
-        row_max(1)
-        keep_positives(0)
-        turn_neg(1)
-        row_max(2)
+        gather_pos(3)
+        cast_x(2)
+        cast_x(3)
+        group_x([2,3],"b2")
+        positive_score(0,"wd0",0)
+        positive_score(1,"wd1",0)
+        direct_scores(0,"b0")
+        direct_scores(1,"b1")
+        scores(1,0,"b3")
+        scores(1,1,"b2")
+        direct_max(0)
+        direct_max(1)
+        positive_score(2,"wd1",1)
+        positive_score(3,"xg2",0)
+        keep_positives([0,1,2],"k0")
+        turn_neg(1,"b4")
+        row_max(2,"b3")
+        row_max(3,"b2")
         factors(0)
-        row_max(3)
-        nc.vector.quantize_mx(
-            out=wi_codes[:].bitcast(E4M3), scales=wi_scales[:], in_=wi_grouped[:].rearrange("s d k -> s (d k)")
-        )
-        gradient(0)
         factors(1)
-        gradient(1)
         factors(2)
-        gradient(2)
         factors(3)
-        multiply(0)
-        gradient(3)
+        gradient(0,"b5")
+        gradient(1,"b6")
+        gradient(2,"b5")
+        gradient(3,"b6")
+        quantise_wi("wi")
+        multiply(0,"b0")
         nc.vector.tensor_tensor(miss[:], e[:, :, I], inv[:], ALU.mult)
-        multiply(1)
+        multiply(1,"b1")
         nc.vector.scalar_tensor_tensor(gp[:], miss[:], -1.0, wt_us_tp[:], ALU.add, ALU.mult)
-        keep_positives(1)
-        keep_positives(2)
-        keep_positives(3)
+        keep_positives([3],"minus_z3")
+        multiply(2,"b3")
+        multiply(3,"b2")
         finish(0)
-        multiply(2)
         finish(1)
-        multiply(3)
         finish(2)
-        finish(3)
+        finish(3,1)

@@ -3,8 +3,8 @@ from contextlib import ExitStack
 import concourse.mybir as mybir
 from concourse.masks import make_identity
 
-R, D, T, I = 512, 512, 2048, 512
-FLOPS = 2 * 2 * R * D * I
+ROWS, FEATURES, ITEMS, SLOTS = 512, 512, 2048, 512
+FLOPS = 2 * 2 * ROWS * FEATURES * SLOTS
 
 F32 = mybir.dt.float32
 BF16 = mybir.dt.bfloat16
@@ -20,11 +20,11 @@ P = 128
 PACK = 4
 TILES = 4
 HALF = 256
+BANK = 512
 LAST = P - 1
-PTAG = "products"
-LATE = ["late0", "late1"]
-PROD = ["wd1", "wd0", "p2", "p3"]
-ORDER = [("w", 0), ("w", 1), ("x", 0), ("x", 1), ("w", 2), ("x", 2), ("w", 3), ("x", 3)]
+LIST_ROWS = 16
+RUN = 4
+MX_ALIGN = 64
 
 
 def tile_attend_gspos_sm_x_kernel(tc, x, wT, us, ts, wt, offs, poffs, out):
@@ -33,308 +33,308 @@ def tile_attend_gspos_sm_x_kernel(tc, x, wT, us, ts, wt, offs, poffs, out):
         keep = ctx.enter_context(tc.tile_pool(name="keep", bufs=1))
         psum = ctx.enter_context(tc.psum_pool(name="psum", bufs=1))
 
-        neg_list = keep.tile([P, I // 16], U16, name="neg_list")
-        pos_list = keep.tile([P, R // 16], U16, name="pos_list")
-        ts_table = keep.tile([P, T], F32, name="ts_table")
-        row_factors = keep.tile([P, R], F32, name="row_factors")
-        planes = [keep.tile([P, T], F32, name=f"plane{t}") for t in range(PACK)]
-        x_rows = [keep.tile([P, D], F32, name=f"x_rows{j}") for j in range(TILES)]
+        def bank_tile(number):
+            return psum.tile([P, BANK], F32, name="bank", tag=f"bank{number}")
+
+        def block(j):
+            return slice(j * P, (j + 1) * P)
+
+        def column(j):
+            return slice(j, j + 1)
+
+        def flat(grouped):
+            return grouped.rearrange("p c t -> p (c t)")
+
+        neg_list = keep.tile([P, SLOTS // LIST_ROWS], U16, name="neg_list")
+        pos_list = keep.tile([P, ROWS // LIST_ROWS], U16, name="pos_list")
+        ts_table = keep.tile([P, ITEMS], F32, name="ts_table")
+        row_factors = keep.tile([P, ROWS], F32, name="row_factors")
+        planes = [keep.tile([P, ITEMS], F32, name=f"plane{t}") for t in range(PACK)]
+        x_rows = [keep.tile([P, FEATURES], F32, name=f"x_rows{j}") for j in range(TILES)]
         ident = keep.tile([P, P], F32, name="ident")
-        warm = keep.tile([P, 1], F32, name="warm")
-        warm2 = keep.tile([P, 1], F32, name="warm2")
 
         wT_planes = wT.rearrange("(p t) c -> t p c", t=PACK)
+
+        def load_plane(t):
+            nc.sync.dma_start(planes[t][:], wT_planes[t])
+
+        def load_x(j):
+            nc.sync.dma_start(x_rows[j][:], x[block(j), :])
+
         nc.sync.dma_start(neg_list[:], offs)
         nc.sync.dma_start(pos_list[:], poffs)
-        for kind, n in ORDER:
-            if kind == "w":
-                nc.sync.dma_start(planes[n][:], wT_planes[n])
-            else:
-                nc.sync.dma_start(x_rows[n][:], x[n * P:(n + 1) * P, :])
+        load_plane(0)
+        load_plane(1)
+        load_x(0)
+        load_x(1)
+        load_plane(2)
+        load_x(2)
+        load_plane(3)
+        load_x(3)
         nc.scalar.dma_start(ts_table[LAST:P, :], ts[0:1, :])
         nc.scalar.dma_start(row_factors[LAST - 1:LAST, :], us.rearrange("r o -> o r"))
         nc.scalar.dma_start(row_factors[LAST:P, :], wt.rearrange("r o -> o r"))
-
-        nc.vector.memset(warm[:], 0.0)
         nc.vector.memset(ts_table[0:LAST, :], 0.0)
-        nc.scalar.activation(warm2[:], warm[:], ACT.Exp)
         make_identity(nc, ident[:])
         nc.gpsimd.memset(row_factors[0:LAST - 1, :], 0.0)
 
-        def turn_bank(name, tag):
-            return psum.tile([P, 512], F32, name=name, tag=tag)
-
-        def turn_row(src, bank):
+        def turn_rows(rows, number):
+            bank = bank_tile(number)
             for j in range(TILES):
-                nc.tensor.transpose(bank[:, j * P:(j + 1) * P], src[:, j * P:(j + 1) * P], ident[:])
+                nc.tensor.transpose(bank[:, block(j)], rows[:, block(j)], ident[:])
+            return bank
 
-        ts_neg_row = keep.tile([P, I], F32, name="ts_neg_row")
-        ts_pos_row = keep.tile([P, R], F32, name="ts_pos_row")
+        ts_neg_row = keep.tile([P, SLOTS], F32, name="ts_neg_row")
+        ts_pos_row = keep.tile([P, ROWS], F32, name="ts_pos_row")
         nc.vector.tensor_copy(ts_neg_row[:], ts_table[:].indirect(neg_list[:]))
         nc.vector.tensor_copy(ts_pos_row[:], ts_table[:].indirect(pos_list[:]))
 
         ts_neg = keep.tile([P, TILES], F32, name="ts_neg")
-        ts_neg_spread = keep.tile([P, I], F32, name="ts_neg_spread", tag="spread", align_bytes=64)
+        ts_neg_spread = keep.tile([P, SLOTS], F32, name="ts_neg_spread")
         us_col = keep.tile([P, TILES], F32, name="us_col")
         minus_us = keep.tile([P, TILES], F32, name="minus_us")
         wt_us = keep.tile([P, TILES], F32, name="wt_us")
         minus_us_tp = keep.tile([P, TILES], F32, name="minus_us_tp")
         wt_us_tp = keep.tile([P, TILES], F32, name="wt_us_tp")
-        bank = turn_bank("uw_bank", "b0")
-        turn_row(row_factors, bank)
-        nc.scalar.copy(us_col[:], bank[:, LAST - 1::P])
-        nc.scalar.mul(minus_us[:], bank[:, LAST - 1::P], -1.0)
-        for j in range(TILES):
-            nc.scalar.mul(wt_us[:, j:j + 1], bank[:, j * P + LAST:(j + 1) * P], us_col[:, j:j + 1])
-        bank = turn_bank("tn_bank", "b1")
-        turn_row(ts_neg_row, bank)
-        nc.scalar.copy(ts_neg[:], bank[:, LAST::P])
-        bank = turn_bank("tp_bank", "b2")
-        turn_row(ts_pos_row, bank)
-        for j in range(TILES):
-            ts_pos = bank[:, j * P + LAST:(j + 1) * P]
-            nc.scalar.mul(minus_us_tp[:, j:j + 1], ts_pos, minus_us[:, j:j + 1])
-            nc.scalar.mul(wt_us_tp[:, j:j + 1], ts_pos, wt_us[:, j:j + 1])
-        bank = turn_bank("spread_bank", "b3")
-        for j in range(TILES):
-            nc.tensor.transpose(bank[:, j * P:(j + 1) * P], ts_neg[:, j:j + 1].to_broadcast([P, P]), ident[:])
-        nc.scalar.copy(ts_neg_spread[:], bank[:])
 
-        w_neg = keep.tile([P, PACK, I], BF16, name="w_neg", align_bytes=64)
-        w_pos = [keep.tile([P, R], F32, name=f"w_pos{t}") for t in range(PACK)]
-        wd_codes = keep.tile([P, I], U32, name="wd_codes", align_bytes=64)
-        wd_scales = keep.tile([P, I], U8, name="wd_scales", align_bytes=64)
-        x_bf = [keep.tile([P, D], BF16, name=f"x_bf{j}", align_bytes=64) for j in range(TILES)]
-        x_codes = keep.tile([P, R], U32, name="x_codes", align_bytes=64)
-        x_scales = keep.tile([P, R], U8, name="x_scales", align_bytes=64)
-        wi_grouped = keep.tile([P, D, PACK], BF16, name="wi_grouped", align_bytes=64)
-        wi_scales = keep.tile([P, D], U8, name="wi_scales", align_bytes=64)
+        turned = turn_rows(row_factors, 0)
+        nc.scalar.copy(us_col[:], turned[:, LAST - 1::P])
+        nc.scalar.mul(minus_us[:], turned[:, LAST - 1::P], -1.0)
+        for j in range(TILES):
+            nc.scalar.mul(wt_us[:, column(j)], turned[:, column(j * P + LAST)], us_col[:, column(j)])
+        turned = turn_rows(ts_neg_row, 1)
+        nc.scalar.copy(ts_neg[:], turned[:, LAST::P])
+        turned = turn_rows(ts_pos_row, 2)
+        for j in range(TILES):
+            ts_pos = turned[:, column(j * P + LAST)]
+            nc.scalar.mul(minus_us_tp[:, column(j)], ts_pos, minus_us[:, column(j)])
+            nc.scalar.mul(wt_us_tp[:, column(j)], ts_pos, wt_us[:, column(j)])
+        turned = bank_tile(3)
+        for j in range(TILES):
+            nc.tensor.transpose(turned[:, block(j)], ts_neg[:, column(j)].to_broadcast([P, P]), ident[:])
+        nc.scalar.copy(ts_neg_spread[:], turned[:])
+
+        w_neg = keep.tile([P, PACK, SLOTS], BF16, name="w_neg", align_bytes=MX_ALIGN)
+        w_pos = [keep.tile([P, ROWS], F32, name=f"w_pos{t}") for t in range(PACK)]
 
         def gather_neg(t, first, count):
-            nc.vector.tensor_copy(
-                w_neg[:, t, first:first + count], planes[t][:].indirect(neg_list[:, first // 16:(first + count) // 16])
-            )
+            offsets = neg_list[:, first // LIST_ROWS:(first + count) // LIST_ROWS]
+            nc.vector.tensor_copy(w_neg[:, t, first:first + count], planes[t][:].indirect(offsets))
 
         def gather_pos(t):
             nc.vector.tensor_copy(w_pos[t][:], planes[t][:].indirect(pos_list[:]))
 
-        def group_wd(h):
-            cols = slice(h * HALF, (h + 1) * HALF)
-            wd_grouped = keep.tile([P, HALF, PACK], BF16, name="wd_grouped", tag=f"wd{h}", align_bytes=64)
-            nc.scalar.copy(
-                wd_grouped[:].rearrange("p (c i) t -> p c t i", i=4),
-                w_neg[:, :, cols].rearrange("p t (c i) -> p c t i", i=4),
-            )
-            nc.vector.quantize_mx(
-                out=wd_codes[:, cols].bitcast(E4M3), scales=wd_scales[:, cols],
-                in_=wd_grouped[:].rearrange("p i t -> p (i t)"),
-            )
+        wd_codes = keep.tile([P, SLOTS], U32, name="wd_codes", align_bytes=MX_ALIGN)
+        wd_scales = keep.tile([P, SLOTS], U8, name="wd_scales", align_bytes=MX_ALIGN)
+        x_bf = [keep.tile([P, FEATURES], BF16, name=f"x_bf{j}", align_bytes=MX_ALIGN) for j in range(TILES)]
+        x_codes = keep.tile([P, ROWS], U32, name="x_codes", align_bytes=MX_ALIGN)
+        x_scales = keep.tile([P, ROWS], U8, name="x_scales", align_bytes=MX_ALIGN)
 
-        def cast_x(j):
+        def quantise_neg_along_d(h):
+            slots = slice(h * HALF, (h + 1) * HALF)
+            grouped = keep.tile([P, HALF, PACK], BF16, name="wd_grouped", tag=f"wd_grouped{h}", align_bytes=MX_ALIGN)
             nc.scalar.copy(
-                x_bf[j][:].rearrange("r (u p e) -> r u p e", u=2, e=2),
-                x_rows[j][:].rearrange("r (p u e) -> r u p e", u=2, e=2),
+                grouped[:].rearrange("p (c i) t -> p c t i", i=RUN),
+                w_neg[:, :, slots].rearrange("p t (c i) -> p c t i", i=RUN),
             )
+            nc.vector.quantize_mx(out=wd_codes[:, slots].bitcast(E4M3), scales=wd_scales[:, slots], in_=flat(grouped[:]))
 
-        def group_x(tiles, tag):
-            bank = psum.tile([P, 512], F32, name="x_bank", tag=tag)
-            n = len(tiles)
-            for rr, j in enumerate(tiles):
-                words = x_bf[j][:].bitcast(F32)
+        def quantise_x(h, number):
+            for j in (2 * h, 2 * h + 1):
+                nc.scalar.copy(
+                    x_bf[j][:].rearrange("r (u p e) -> r u p e", u=2, e=2),
+                    x_rows[j][:].rearrange("r (p u e) -> r u p e", u=2, e=2),
+                )
+            bank = bank_tile(number)
+            for a in range(2):
+                words = x_bf[2 * h + a][:].bitcast(F32)
                 for u in range(2):
-                    nc.tensor.transpose(bank[:, (2 * rr + u) * P:(2 * rr + u + 1) * P], words[:, u * P:(u + 1) * P], ident[:])
-            rows = slice(tiles[0] * P, (tiles[0] + n) * P)
-            x_grouped = keep.tile([P, n * P, PACK], BF16, name="x_grouped", tag=f"xg{tiles[0]}", align_bytes=64)
+                    nc.tensor.transpose(bank[:, block(2 * a + u)], words[:, block(u)], ident[:])
+            rows = slice(h * HALF, (h + 1) * HALF)
+            grouped = keep.tile([P, HALF, PACK], BF16, name="x_grouped", tag=f"x_grouped{h}", align_bytes=MX_ALIGN)
             nc.scalar.copy(
-                x_grouped[:].rearrange("p r t -> p (r t)").bitcast(F32).rearrange("p (a r u) -> p a r u", a=n, u=2),
-                bank[:, 0:n * HALF].rearrange("p (a u r) -> p a r u", a=n, u=2),
+                flat(grouped[:]).bitcast(F32).rearrange("p (a r u) -> p a r u", a=2, u=2),
+                bank[:].rearrange("p (a u r) -> p a r u", a=2, u=2),
             )
-            nc.vector.quantize_mx(
-                out=x_codes[:, rows].bitcast(E4M3), scales=x_scales[:, rows],
-                in_=x_grouped[:].rearrange("p r t -> p (r t)"),
-            )
+            nc.vector.quantize_mx(out=x_codes[:, rows].bitcast(E4M3), scales=x_scales[:, rows], in_=flat(grouped[:]))
 
-        def turn_neg(m, tag):
+        wi_grouped = keep.tile([P, FEATURES, PACK], BF16, name="wi_grouped", align_bytes=MX_ALIGN)
+        wi_codes = keep.tile([P, FEATURES], U32, name="wi_codes", align_bytes=MX_ALIGN)
+        wi_scales = keep.tile([P, FEATURES], U8, name="wi_scales", align_bytes=MX_ALIGN)
+
+        def turn_neg(m, number):
             words = w_neg[:].rearrange("p t i -> p (t i)").bitcast(F32).rearrange("p (t w) -> p t w", t=PACK)
-            wi_words = wi_grouped[:].rearrange("s d k -> s (d k)").bitcast(F32).rearrange(
-                "s (p t u) -> s p t u", t=PACK, u=2)
-            bank = psum.tile([P, 512], F32, name="wi_bank", tag=tag)
+            wi_words = flat(wi_grouped[:]).bitcast(F32).rearrange("s (p t u) -> s p t u", t=PACK, u=2)
+            bank = bank_tile(number)
             for a in reversed(range(2)):
                 for u in range(2):
-                    nc.tensor.transpose(bank[:, (2 * a + u) * P:(2 * a + u + 1) * P], words[:, 2 * m + a, u::2], ident[:])
+                    nc.tensor.transpose(bank[:, block(2 * a + u)], words[:, 2 * m + a, u::2], ident[:])
             nc.scalar.copy(wi_words[:, :, 2 * m:2 * m + 2, :], bank[:].rearrange("s (a u p) -> s p a u", a=2, u=2))
 
-        scaled_T = [keep.tile([P, TILES, HALF], F32, name=f"scaled_T{h}", tag=f"late{h}") for h in range(2)]
+        def quantise_neg_along_i():
+            nc.vector.quantize_mx(out=wi_codes[:].bitcast(E4M3), scales=wi_scales[:], in_=flat(wi_grouped[:]))
 
-        def scores(h, jj, tag):
-            rows = slice(h * HALF, (h + 1) * HALF)
-            acc = psum.tile([P, 2, HALF], F32, name="acc", tag=tag)
-            for a in range(2):
-                slots = slice((2 * jj + a) * P, (2 * jj + a + 1) * P)
-                nc.tensor.matmul_mx(
-                    out=acc[:, a, :], lhsT=wd_codes[:, slots].bitcast(E4M3), lhsT_scale=wd_scales[:, slots],
-                    rhs=x_codes[:, rows].bitcast(E4M3), rhs_scale=x_scales[:, rows], start=True, stop=True,
-                )
-            for a in range(2):
-                j = 2 * jj + a
-                nc.scalar.activation(scaled_T[h][:, j, :], acc[:, a, :], ACT.Copy, scale=ts_neg[:, j:j + 1])
-
-        minus_z = [keep.tile([P, I + 1], F32, name=f"minus_z{j}", tag=f"minus_z{j}") for j in range(TILES)]
-        e = keep.tile([P, TILES, I + 8], F32, name="e")
-        g = [keep.tile([P, I], BF16, name=f"g{j}", align_bytes=64) for j in range(TILES)]
+        minus_z = [keep.tile([P, SLOTS + 1], F32, name=f"minus_z{j}", tag=f"minus_z{j}") for j in range(TILES)]
+        e = keep.tile([P, TILES, SLOTS + 8], F32, name="e")
         minus_m = keep.tile([P, TILES], F32, name="minus_m")
         tot = keep.tile([P, TILES], F32, name="tot")
         inv = keep.tile([P, TILES], F32, name="inv")
-        c = keep.tile([P, TILES], F32, name="c")
+        wt_us_inv = keep.tile([P, TILES], F32, name="wt_us_inv")
+        pos_share = keep.tile([P, TILES], F32, name="pos_share")
         gp = keep.tile([P, TILES], F32, name="gp")
-        miss = keep.tile([P, TILES], F32, name="miss")
-
+        scaled_T = keep.tile([P, TILES, HALF], F32, name="scaled_T")
         pos_banks = {}
-        junk = {}
-
-        def positive_score(j, tag, n):
-            bank = turn_bank(f"pos_bank{j}", f"b{4 + j}")
-            for t in (2, 0, 1, 3):
-                nc.tensor.transpose(bank[:, t * P:(t + 1) * P], w_pos[t][:, j * P:(j + 1) * P], ident[:])
-            pos_banks[j] = bank[:].rearrange("r (t p) -> r p t", t=PACK)
-            if tag not in junk:
-                junk[tag] = keep.tile([P, 2, D], F32, name="products", tag=tag, align_bytes=64)
-            products = junk[tag][:, n, :]
-            nc.vector.scalar_tensor_tensor(
-                products.rearrange("r (p t) -> r p t", t=PACK), pos_banks[j], minus_us_tp[:, j:j + 1],
-                x_rows[j][:].rearrange("r (p t) -> r p t", t=PACK), ALU.mult, ALU.mult,
-                accum_out=minus_z[j][:, I:I + 1],
-            )
-
         w_pos_rows = {}
 
+        def spent(tag, count):
+            return keep.tile([P, count, FEATURES], F32, name="products", tag=tag, align_bytes=MX_ALIGN)
+
+        def positive_score(j, products):
+            bank = bank_tile(TILES + j)
+            for t in (2, 0, 1, 3):
+                nc.tensor.transpose(bank[:, t::PACK], w_pos[t][:, block(j)], ident[:])
+            pos_banks[j] = bank
+            nc.vector.scalar_tensor_tensor(
+                products, bank[:], minus_us_tp[:, column(j)], x_rows[j][:], ALU.mult, ALU.mult,
+                accum_out=minus_z[j][:, column(SLOTS)],
+            )
+
         def keep_positives(tiles, tag):
-            kept = keep.tile([P, len(tiles), D], F32, name="w_pos_rows", tag=tag)
+            kept = keep.tile([P, len(tiles), FEATURES], F32, name="w_pos_rows", tag=tag)
             for n, j in enumerate(tiles):
                 w_pos_rows[j] = kept[:, n, :]
-                nc.scalar.copy(w_pos_rows[j].rearrange("r (p t) -> r p t", t=PACK), pos_banks[j])
+                nc.scalar.copy(w_pos_rows[j], pos_banks[j][:])
 
-        def direct_scores(j, tag):
-            rows = slice(j * P, (j + 1) * P)
-            acc = psum.tile([P, I], F32, name="a", tag=tag)
+        def scores_by_row(j, number):
+            a = bank_tile(number)
             nc.tensor.matmul_mx(
-                out=acc[:], lhsT=x_codes[:, rows].bitcast(E4M3), lhsT_scale=x_scales[:, rows],
+                out=a[:], lhsT=x_codes[:, block(j)].bitcast(E4M3), lhsT_scale=x_scales[:, block(j)],
                 rhs=wd_codes[:].bitcast(E4M3), rhs_scale=wd_scales[:], start=True, stop=True,
             )
-            nc.vector.scalar_tensor_tensor(minus_z[j][:, 0:I], acc[:], minus_us[:, j:j + 1], ts_neg_spread[:], ALU.mult, ALU.mult)
+            nc.vector.scalar_tensor_tensor(
+                minus_z[j][:, 0:SLOTS], a[:], minus_us[:, column(j)], ts_neg_spread[:], ALU.mult, ALU.mult
+            )
 
-        def direct_max(j):
-            col = slice(j, j + 1)
-            nc.vector.tensor_reduce(minus_m[:, col], minus_z[j][:], mybir.AxisListType.X, ALU.min)
-            nc.scalar.activation(e[:, j, 0:I + 1], minus_z[j][:], ACT.Exp, bias=minus_m[:, col], scale=-1.0, accum_out=tot[:, col])
+        def scores_by_slot(h, number):
+            a_T = bank_tile(number)
+            for n in range(2):
+                slots = block(2 * h + n)
+                nc.tensor.matmul_mx(
+                    out=a_T[:, n * HALF:(n + 1) * HALF], lhsT=wd_codes[:, slots].bitcast(E4M3), lhsT_scale=wd_scales[:, slots],
+                    rhs=x_codes[:, HALF:ROWS].bitcast(E4M3), rhs_scale=x_scales[:, HALF:ROWS], start=True, stop=True,
+                )
+            for n in range(2):
+                s = 2 * h + n
+                nc.scalar.activation(scaled_T[:, s, :], a_T[:, n * HALF:(n + 1) * HALF], ACT.Copy, scale=ts_neg[:, column(s)])
 
-        def row_max(j, tag):
-            h, rr = divmod(j, 2)
-            y = psum.tile([P, I], F32, name="y", tag=tag)
+        def exponentials(j):
+            nc.scalar.activation(
+                e[:, j, 0:SLOTS + 1], minus_z[j][:], ACT.Exp, bias=minus_m[:, column(j)], scale=-1.0,
+                accum_out=tot[:, column(j)],
+            )
+
+        def softmax_by_row(j):
+            nc.vector.tensor_reduce(minus_m[:, column(j)], minus_z[j][:], mybir.AxisListType.X, ALU.min)
+            exponentials(j)
+
+        def softmax_by_slot(j, number):
+            scaled = bank_tile(number)
             for s in range(TILES):
-                nc.tensor.transpose(y[:, s * P:(s + 1) * P], scaled_T[h][:, s, rr * P:(rr + 1) * P], ident[:])
-            col = slice(j, j + 1)
+                nc.tensor.transpose(scaled[:, block(s)], scaled_T[:, s, block(j - 2)], ident[:])
             nc.vector.tensor_scalar(
-                minus_z[j][:, 0:I], y[:], minus_us[:, col], minus_z[j][:, I:I + 1], ALU.mult, ALU.min, accum_out=minus_m[:, col]
+                minus_z[j][:, 0:SLOTS], scaled[:], minus_us[:, column(j)], minus_z[j][:, column(SLOTS)], ALU.mult, ALU.min,
+                accum_out=minus_m[:, column(j)],
             )
-            nc.scalar.activation(e[:, j, 0:I + 1], minus_z[j][:], ACT.Exp, bias=minus_m[:, col], scale=-1.0, accum_out=tot[:, col])
+            exponentials(j)
 
-        g_grouped = [keep.tile([P, P, PACK], BF16, name=f"g_grouped{j}", align_bytes=64) for j in range(TILES)]
-        g_codes = [keep.tile([P, P], U32, name=f"g_codes{j}", align_bytes=64) for j in range(TILES)]
-        g_scales = [keep.tile([P, P], U8, name=f"g_scales{j}", align_bytes=64) for j in range(TILES)]
+        def row_factor(j):
+            nc.vector.reciprocal(inv[:, column(j)], tot[:, column(j)])
+            nc.scalar.mul(wt_us_inv[:, column(j)], inv[:, column(j)], wt_us[:, column(j)])
 
-        def factors(j):
-            col = slice(j, j + 1)
-            nc.vector.reciprocal(inv[:, col], tot[:, col])
-            nc.scalar.mul(c[:, col], inv[:, col], wt_us[:, col])
-
-        def gradient(j, tag):
-            col = slice(j, j + 1)
-            nc.vector.scalar_tensor_tensor(g[j][:], e[:, j, 0:I], c[:, col], ts_neg_spread[:], ALU.mult, ALU.mult)
-            bank = psum.tile([P, 512], F32, name=f"g_bank{j}", tag=tag)
-            words = g[j][:].bitcast(F32)
-            for u in range(2):
-                nc.tensor.transpose(bank[:, u * P:(u + 1) * P], words[:, u::2], ident[:])
-            nc.scalar.copy(
-                g_grouped[j][:].rearrange("p r t -> p (r t)").bitcast(F32).rearrange("p (r u) -> p r u", u=2),
-                bank[:, 0:2 * P].rearrange("p (u r) -> p r u", u=2),
-            )
-
-        wi = {}
-
-        def quantise_wi(tag):
-            wi[0] = keep.tile([P, D], U32, name="wi_codes", tag=tag, align_bytes=64)
-            nc.vector.quantize_mx(out=wi[0][:].bitcast(E4M3), scales=wi_scales[:], in_=wi_grouped[:].rearrange("s d k -> s (d k)"))
-
-        result = [keep.tile([P, D], F32, name=f"result{j}") for j in range(TILES)]
+        g = [keep.tile([P, SLOTS], BF16, name=f"g{j}", align_bytes=MX_ALIGN) for j in range(TILES)]
+        g_grouped = [keep.tile([P, P, PACK], BF16, name=f"g_grouped{j}", align_bytes=MX_ALIGN) for j in range(TILES)]
+        g_codes = [keep.tile([P, P], U32, name=f"g_codes{j}", align_bytes=MX_ALIGN) for j in range(TILES)]
+        g_scales = [keep.tile([P, P], U8, name=f"g_scales{j}", align_bytes=MX_ALIGN) for j in range(TILES)]
+        result = [keep.tile([P, FEATURES], F32, name=f"result{j}") for j in range(TILES)]
         gx = {}
 
-        def multiply(j, tag):
-            nc.vector.quantize_mx(
-                out=g_codes[j][:].bitcast(E5M2), scales=g_scales[j][:], in_=g_grouped[j][:].rearrange("p r t -> p (r t)")
+        def gradient(j, number):
+            nc.vector.scalar_tensor_tensor(
+                g[j][:], e[:, j, 0:SLOTS], wt_us_inv[:, column(j)], ts_neg_spread[:], ALU.mult, ALU.mult
             )
-            gx[j] = psum.tile([P, D], F32, name="gx", tag=tag)
+            bank = bank_tile(number)
+            words = g[j][:].bitcast(F32)
+            for u in range(2):
+                nc.tensor.transpose(bank[:, block(u)], words[:, u::2], ident[:])
+            nc.scalar.copy(
+                flat(g_grouped[j][:]).bitcast(F32).rearrange("p (r u) -> p r u", u=2),
+                bank[:, 0:HALF].rearrange("p (u r) -> p r u", u=2),
+            )
+
+        def multiply(j, number):
+            nc.vector.quantize_mx(out=g_codes[j][:].bitcast(E5M2), scales=g_scales[j][:], in_=flat(g_grouped[j][:]))
+            gx[j] = bank_tile(number)
             nc.tensor.matmul_mx(
                 out=gx[j][:], lhsT=g_codes[j][:].bitcast(E5M2), lhsT_scale=g_scales[j][:],
-                rhs=wi[0][:].bitcast(E4M3), rhs_scale=wi_scales[:], start=True, stop=True,
+                rhs=wi_codes[:].bitcast(E4M3), rhs_scale=wi_scales[:], start=True, stop=True,
             )
 
-        def finish(j, pieces=1):
-            width = D // pieces
+        def finish(j, pieces):
+            width = FEATURES // pieces
             for n in range(pieces):
                 cols = slice(n * width, (n + 1) * width)
-                nc.vector.scalar_tensor_tensor(result[j][:, cols], w_pos_rows[j][:, cols], gp[:, j:j + 1], gx[j][:, cols], ALU.mult, ALU.add)
-                nc.sync.dma_start(out[j * P:(j + 1) * P, cols], result[j][:, cols])
+                nc.vector.scalar_tensor_tensor(
+                    result[j][:, cols], w_pos_rows[j][:, cols], gp[:, column(j)], gx[j][:, cols], ALU.mult, ALU.add
+                )
+                nc.sync.dma_start(out[block(j), cols], result[j][:, cols])
 
-        gather_neg(0, 0, I)
-        gather_pos(0)
-        gather_neg(1, 0, I)
-        gather_pos(1)
-        turn_neg(0,"b0")
-        gather_neg(2, 0, I)
-        gather_pos(2)
-        gather_neg(3, 0, HALF)
-        gather_neg(3, HALF, HALF)
-        cast_x(0)
-        cast_x(1)
-        group_x([0,1],"b1")
-        group_wd(0)
-        group_wd(1)
-        gather_pos(3)
-        cast_x(2)
-        cast_x(3)
-        group_x([2,3],"b2")
-        positive_score(0,"wd0",0)
-        positive_score(1,"wd1",0)
-        direct_scores(0,"b0")
-        direct_scores(1,"b1")
-        scores(1,0,"b3")
-        scores(1,1,"b2")
-        direct_max(0)
-        direct_max(1)
-        positive_score(2,"wd1",1)
-        positive_score(3,"xg2",0)
-        keep_positives([0,1,2],"k0")
-        turn_neg(1,"b4")
-        row_max(2,"b3")
-        row_max(3,"b2")
-        factors(0)
-        factors(1)
-        factors(2)
-        factors(3)
-        gradient(0,"b5")
-        gradient(1,"b6")
-        gradient(2,"b5")
-        gradient(3,"b6")
-        quantise_wi("wi")
-        multiply(0,"b0")
-        nc.vector.tensor_tensor(miss[:], e[:, :, I], inv[:], ALU.mult)
-        multiply(1,"b1")
-        nc.vector.scalar_tensor_tensor(gp[:], miss[:], -1.0, wt_us_tp[:], ALU.add, ALU.mult)
-        keep_positives([3],"minus_z3")
-        multiply(2,"b3")
-        multiply(3,"b2")
-        finish(0)
-        finish(1)
-        finish(2)
-        finish(3,1)
+        for t in range(PACK - 1):
+            gather_neg(t, 0, SLOTS)
+            gather_pos(t)
+            if t == 1:
+                turn_neg(0, 0)
+        gather_neg(PACK - 1, 0, HALF)
+        gather_neg(PACK - 1, HALF, HALF)
+        quantise_x(0, 1)
+        quantise_neg_along_d(0)
+        quantise_neg_along_d(1)
+        gather_pos(PACK - 1)
+        quantise_x(1, 2)
+
+        behind_first_half = spent("wd_grouped0", 1)
+        behind_second_half = spent("wd_grouped1", 2)
+        behind_x = spent("x_grouped1", 1)
+        positive_score(0, behind_first_half[:, 0, :])
+        positive_score(1, behind_second_half[:, 0, :])
+        scores_by_row(0, 0)
+        scores_by_row(1, 1)
+        scores_by_slot(0, 3)
+        scores_by_slot(1, 2)
+        softmax_by_row(0)
+        softmax_by_row(1)
+        positive_score(2, behind_second_half[:, 1, :])
+        positive_score(3, behind_x[:, 0, :])
+        keep_positives([0, 1, 2], "w_pos_rows")
+        turn_neg(1, 4)
+
+        row_factor(0)
+        softmax_by_slot(2, 3)
+        row_factor(1)
+        softmax_by_slot(3, 2)
+        row_factor(2)
+        gradient(0, 5)
+        row_factor(3)
+        gradient(1, 6)
+        gradient(2, 5)
+        gradient(3, 6)
+        quantise_neg_along_i()
+
+        multiply(0, 0)
+        nc.vector.tensor_tensor(pos_share[:], e[:, :, SLOTS], inv[:], ALU.mult)
+        multiply(1, 1)
+        nc.vector.scalar_tensor_tensor(gp[:], pos_share[:], -1.0, wt_us_tp[:], ALU.add, ALU.mult)
+        keep_positives([3], "minus_z3")
+        multiply(2, 3)
+        multiply(3, 2)
+        for j in range(TILES):
+            finish(j, 2 if j == TILES - 1 else 1)

@@ -141,9 +141,10 @@ def tile_attend_gspos_sm_x_kernel(tc, x, wT, us, ts, wt, offs, poffs, out):
 
         def quantise_x(h, number):
             for j in (2 * h, 2 * h + 1):
-                nc.scalar.copy(
+                nc.gpsimd.tensor_scalar(
                     x_bf[j][:].rearrange("r (u p e) -> r u p e", u=2, e=2),
                     x_rows[j][:].rearrange("r (p u e) -> r u p e", u=2, e=2),
+                    1.0, 0.0, ALU.mult, ALU.add,
                 )
             bank = bank_tile(number)
             for a in range(2):

@@ -160,7 +160,6 @@ def tile_attend_gspos_sm_x_kernel(tc, x, wT, us, ts, wt, offs, poffs, out):
             nc.vector.quantize_mx(out=x_codes[:, rows].bitcast(E4M3), scales=x_scales[:, rows], in_=flat(grouped[:]))
 
         wi_grouped = keep.tile([P, FEATURES, PACK], BF16, name="wi_grouped", align_bytes=MX_ALIGN)
-        wi_codes = keep.tile([P, FEATURES], U32, name="wi_codes", align_bytes=MX_ALIGN)
         wi_scales = keep.tile([P, FEATURES], U8, name="wi_scales", align_bytes=MX_ALIGN)
 
         def turn_neg(m, number):
@@ -175,15 +174,13 @@ def tile_attend_gspos_sm_x_kernel(tc, x, wT, us, ts, wt, offs, poffs, out):
         def quantise_neg_along_i():
             nc.vector.quantize_mx(out=wi_codes[:].bitcast(E4M3), scales=wi_scales[:], in_=flat(wi_grouped[:]))
 
-        minus_z = [keep.tile([P, SLOTS + 1], F32, name=f"minus_z{j}", tag=f"minus_z{j}") for j in range(TILES)]
+        minus_z = [keep.tile([P, SLOTS + 1], F32, name=f"minus_z{j}", tag=f"minus_z{j}", align_bytes=MX_ALIGN) for j in range(TILES)]
         e = keep.tile([P, TILES, SLOTS + 8], F32, name="e")
         minus_m = keep.tile([P, TILES], F32, name="minus_m")
         tot = keep.tile([P, TILES], F32, name="tot")
         inv = keep.tile([P, TILES], F32, name="inv")
-        wt_us_inv = keep.tile([P, TILES], F32, name="wt_us_inv")
         pos_share = keep.tile([P, TILES], F32, name="pos_share")
-        gp = keep.tile([P, TILES], F32, name="gp")
-        scaled_T = keep.tile([P, TILES, HALF], F32, name="scaled_T")
+        scaled_T = [keep.tile([P, TILES, HALF], F32, name=f"scaled_T{r}") for r in range(2)]
         pos_banks = {}
         w_pos_rows = {}
 
@@ -200,33 +197,26 @@ def tile_attend_gspos_sm_x_kernel(tc, x, wT, us, ts, wt, offs, poffs, out):
                 accum_out=minus_z[j][:, column(SLOTS)],
             )
 
-        def keep_positives(tiles, tag):
-            kept = keep.tile([P, len(tiles), FEATURES], F32, name="w_pos_rows", tag=tag)
-            for n, j in enumerate(tiles):
-                w_pos_rows[j] = kept[:, n, :]
-                nc.scalar.copy(w_pos_rows[j], pos_banks[j][:])
+        def keep_positives(j, tag):
+            w_pos_rows[j] = keep.tile([P, FEATURES], F32, name="w_pos_rows", tag=tag, align_bytes=MX_ALIGN)
+            nc.scalar.mul(w_pos_rows[j][:], pos_banks[j][:], wt_us_tp[:, column(j)])
 
-        def scores_by_row(j, number):
-            a = bank_tile(number)
-            nc.tensor.matmul_mx(
-                out=a[:], lhsT=x_codes[:, block(j)].bitcast(E4M3), lhsT_scale=x_scales[:, block(j)],
-                rhs=wd_codes[:].bitcast(E4M3), rhs_scale=wd_scales[:], start=True, stop=True,
-            )
-            nc.vector.scalar_tensor_tensor(
-                minus_z[j][:, 0:SLOTS], a[:], minus_us[:, column(j)], ts_neg_spread[:], ALU.mult, ALU.mult
+        def positive_share(j):
+            nc.scalar.activation(
+                pos_share[:, column(j)], e[:, j, column(SLOTS)], ACT.Identity, scale=inv[:, column(j)], bias=-1.0
             )
 
-        def scores_by_slot(h, number):
+        def scores_by_slot(h, rows, number):
             a_T = bank_tile(number)
             for n in range(2):
                 slots = block(2 * h + n)
                 nc.tensor.matmul_mx(
                     out=a_T[:, n * HALF:(n + 1) * HALF], lhsT=wd_codes[:, slots].bitcast(E4M3), lhsT_scale=wd_scales[:, slots],
-                    rhs=x_codes[:, HALF:ROWS].bitcast(E4M3), rhs_scale=x_scales[:, HALF:ROWS], start=True, stop=True,
+                    rhs=x_codes[:, rows * HALF:(rows + 1) * HALF].bitcast(E4M3), rhs_scale=x_scales[:, rows * HALF:(rows + 1) * HALF], start=True, stop=True,
                 )
             for n in range(2):
                 s = 2 * h + n
-                nc.scalar.activation(scaled_T[:, s, :], a_T[:, n * HALF:(n + 1) * HALF], ACT.Copy, scale=ts_neg[:, column(s)])
+                nc.scalar.activation(scaled_T[rows][:, s, :], a_T[:, n * HALF:(n + 1) * HALF], ACT.Copy, scale=ts_neg[:, column(s)])
 
         def exponentials(j):
             nc.scalar.activation(
@@ -234,14 +224,10 @@ def tile_attend_gspos_sm_x_kernel(tc, x, wT, us, ts, wt, offs, poffs, out):
                 accum_out=tot[:, column(j)],
             )
 
-        def softmax_by_row(j):
-            nc.vector.tensor_reduce(minus_m[:, column(j)], minus_z[j][:], mybir.AxisListType.X, ALU.min)
-            exponentials(j)
-
         def softmax_by_slot(j, number):
             scaled = bank_tile(number)
             for s in range(TILES):
-                nc.tensor.transpose(scaled[:, block(s)], scaled_T[:, s, block(j - 2)], ident[:])
+                nc.tensor.transpose(scaled[:, block(s)], scaled_T[j // 2][:, s, block(j % 2)], ident[:])
             nc.vector.tensor_scalar(
                 minus_z[j][:, 0:SLOTS], scaled[:], minus_us[:, column(j)], minus_z[j][:, column(SLOTS)], ALU.mult, ALU.min,
                 accum_out=minus_m[:, column(j)],
@@ -250,9 +236,8 @@ def tile_attend_gspos_sm_x_kernel(tc, x, wT, us, ts, wt, offs, poffs, out):
 
         def row_factor(j):
             nc.vector.reciprocal(inv[:, column(j)], tot[:, column(j)])
-            nc.scalar.mul(wt_us_inv[:, column(j)], inv[:, column(j)], wt_us[:, column(j)])
 
-        g = [keep.tile([P, SLOTS], BF16, name=f"g{j}", align_bytes=MX_ALIGN) for j in range(TILES)]
+        g = [keep.tile([P, SLOTS], BF16, name="g", tag=f"g{j}", align_bytes=MX_ALIGN) for j in range(TILES)]
         g_grouped = [keep.tile([P, P, PACK], BF16, name=f"g_grouped{j}", align_bytes=MX_ALIGN) for j in range(TILES)]
         g_codes = [keep.tile([P, P], U32, name=f"g_codes{j}", align_bytes=MX_ALIGN) for j in range(TILES)]
         g_scales = [keep.tile([P, P], U8, name=f"g_scales{j}", align_bytes=MX_ALIGN) for j in range(TILES)]
@@ -261,7 +246,7 @@ def tile_attend_gspos_sm_x_kernel(tc, x, wT, us, ts, wt, offs, poffs, out):
 
         def gradient(j, number):
             nc.vector.scalar_tensor_tensor(
-                g[j][:], e[:, j, 0:SLOTS], wt_us_inv[:, column(j)], ts_neg_spread[:], ALU.mult, ALU.mult
+                g[j][:], e[:, j, 0:SLOTS], inv[:, column(j)], wt_us_ts[:, j, :], ALU.mult, ALU.mult
             )
             bank = bank_tile(number)
             words = g[j][:].bitcast(F32)
@@ -285,7 +270,7 @@ def tile_attend_gspos_sm_x_kernel(tc, x, wT, us, ts, wt, offs, poffs, out):
             for n in range(pieces):
                 cols = slice(n * width, (n + 1) * width)
                 nc.vector.scalar_tensor_tensor(
-                    result[j][:, cols], w_pos_rows[j][:, cols], gp[:, column(j)], gx[j][:, cols], ALU.mult, ALU.add
+                    result[j][:, cols], w_pos_rows[j][:, cols], pos_share[:, column(j)], gx[j][:, cols], ALU.mult, ALU.add
                 )
                 nc.sync.dma_start(out[block(j), cols], result[j][:, cols])
 
@@ -303,39 +288,34 @@ def tile_attend_gspos_sm_x_kernel(tc, x, wT, us, ts, wt, offs, poffs, out):
         quantise_x(1, 2)
 
         behind_first_half = spent("wd_grouped0", 1)
-        behind_second_half = spent("wd_grouped1", 2)
-        behind_x = spent("x_grouped1", 1)
+        behind_second_half = spent("wd_grouped1", 3)
+        wt_us_ts = keep.tile([P, TILES, SLOTS], F32, name="wt_us_ts", tag="x_grouped1", align_bytes=MX_ALIGN)
+        for j in range(TILES):
+            nc.gpsimd.tensor_scalar(wt_us_ts[:, j, :], ts_neg_spread[:], wt_us[:, column(j)], 0.0, ALU.mult, ALU.add)
+        banks = (0, 1, 3, 2)
+        scores_by_slot(0, 0, banks[0])
+        scores_by_slot(1, 0, banks[1])
+        scores_by_slot(0, 1, banks[2])
+        scores_by_slot(1, 1, banks[3])
         positive_score(0, behind_first_half[:, 0, :])
         positive_score(1, behind_second_half[:, 0, :])
-        scores_by_row(0, 0)
-        scores_by_row(1, 1)
-        scores_by_slot(0, 3)
-        scores_by_slot(1, 2)
-        softmax_by_row(0)
-        softmax_by_row(1)
         positive_score(2, behind_second_half[:, 1, :])
-        positive_score(3, behind_x[:, 0, :])
-        keep_positives([0, 1, 2], "w_pos_rows")
-        turn_neg(1, 4)
-
-        row_factor(0)
-        softmax_by_slot(2, 3)
-        row_factor(1)
-        softmax_by_slot(3, 2)
-        row_factor(2)
-        gradient(0, 5)
-        row_factor(3)
-        gradient(1, 6)
-        gradient(2, 5)
-        gradient(3, 6)
+        positive_score(3, behind_second_half[:, 2, :])
+        for j in range(TILES):
+            softmax_by_slot(j, banks[j])
+            if j >= 2:
+                row_factor(j - 2)
+        turn_neg(1, banks[3])
+        for j in range(TILES):
+            gradient(j, banks[j])
+            if j < 2:
+                row_factor(j + 2)
+        wi_codes = keep.tile([P, FEATURES], U32, name="wi_codes", tag="x_grouped1", align_bytes=MX_ALIGN)
         quantise_neg_along_i()
-
-        multiply(0, 0)
-        nc.vector.tensor_tensor(pos_share[:], e[:, :, SLOTS], inv[:], ALU.mult)
-        multiply(1, 1)
-        nc.vector.scalar_tensor_tensor(gp[:], pos_share[:], -1.0, wt_us_tp[:], ALU.add, ALU.mult)
-        keep_positives([3], "minus_z3")
-        multiply(2, 3)
-        multiply(3, 2)
+        for j, tag in enumerate(("w_pos_rows", "minus_z3", "g1", "g3")):
+            keep_positives(j, tag)
+            positive_share(j)
+        for j in range(TILES):
+            multiply(j, banks[j])
         for j in range(TILES):
             finish(j, 2 if j == TILES - 1 else 1)

@@ -68,8 +68,8 @@ def tile_attend_gspos_sm_x_kernel(tc, x, wT, us, ts, wt, offs, poffs, out):
         load_x(0)
         load_x(1)
         load_plane(2)
-        load_x(2)
         load_plane(3)
+        load_x(2)
         load_x(3)
         nc.scalar.dma_start(ts_table[LAST:P, :], ts[0:1, :])
         nc.scalar.dma_start(row_factors[LAST - 1:LAST, :], us.rearrange("r o -> o r"))

@@ -275,7 +275,12 @@ def tile_attend_gspos_sm_x_kernel(tc, x, wT, us, ts, wt, offs, poffs, out):
                 nc.sync.dma_start(out[block(j), cols], result[j][:, cols])
 
         for t in range(PACK - 1):
-            gather_neg(t, 0, SLOTS)
+            if t == 0:
+                rounded_plane = keep.tile([P, ITEMS], BF16, name="rounded_plane")
+                nc.scalar.activation(rounded_plane[:], planes[t][:], ACT.Copy)
+                nc.scalar.activation(w_neg[:, t, :], rounded_plane[:].indirect(neg_list[:]), ACT.Copy)
+            else:
+                gather_neg(t, 0, SLOTS)
             gather_pos(t)
             if t == 1:
                 turn_neg(0, 0)

@@ -290,7 +290,7 @@ def tile_attend_gspos_sm_x_kernel(tc, x, wT, us, ts, wt, offs, poffs, out):
         quantise_neg_along_d(0)
         quantise_neg_along_d(1)
         gather_pos(PACK - 1)
-        quantise_x(1, 2)
+        quantise_x(1, 7)
 
         behind_first_half = spent("wd_grouped0", 1)
         behind_second_half = spent("wd_grouped1", 3)

@@ -23,14 +23,17 @@ HALF = 256
 BANK = 512
 LAST = P - 1
 LIST_ROWS = 16
-RUN = 4
 MX_ALIGN = 64
+ROOM = 2048
+RUN = 4
+PADDED = SLOTS + 8
 
 
 def tile_attend_gspos_sm_x_kernel(tc, x, wT, us, ts, wt, offs, poffs, out):
     nc = tc.nc
     with ExitStack() as ctx:
         keep = ctx.enter_context(tc.tile_pool(name="keep", bufs=1))
+        shared = ctx.enter_context(tc.tile_pool(name="shared", bufs=1))
         psum = ctx.enter_context(tc.psum_pool(name="psum", bufs=1))
 
         def bank_tile(number):
@@ -38,6 +41,9 @@ def tile_attend_gspos_sm_x_kernel(tc, x, wT, us, ts, wt, offs, poffs, out):
 
         def block(j):
             return slice(j * P, (j + 1) * P)
+
+        def half(h):
+            return slice(h * HALF, (h + 1) * HALF)
 
         def column(j):
             return slice(j, j + 1)
@@ -49,11 +55,14 @@ def tile_attend_gspos_sm_x_kernel(tc, x, wT, us, ts, wt, offs, poffs, out):
         pos_list = keep.tile([P, ROWS // LIST_ROWS], U16, name="pos_list")
         ts_table = keep.tile([P, ITEMS], F32, name="ts_table")
         row_factors = keep.tile([P, ROWS], F32, name="row_factors")
-        planes = [keep.tile([P, ITEMS], F32, name=f"plane{t}") for t in range(PACK)]
-        x_rows = [keep.tile([P, FEATURES], F32, name=f"x_rows{j}") for j in range(TILES)]
+        planes = [keep.tile([P, ITEMS], F32, name=f"plane{t}") for t in range(PACK - 1)]
+        x_rows = [keep.tile([P, FEATURES], F32, name=f"x_rows{j}") for j in range(TILES - 1)]
         ident = keep.tile([P, P], F32, name="ident")
 
         wT_planes = wT.rearrange("(p t) c -> t p c", t=PACK)
+        nc.sync.dma_start(ts_table[LAST:P, :], ts[0:1, :])
+        nc.sync.dma_start(neg_list[:], offs)
+        nc.sync.dma_start(pos_list[:], poffs)
 
         def load_plane(t):
             nc.sync.dma_start(planes[t][:], wT_planes[t])
@@ -61,22 +70,41 @@ def tile_attend_gspos_sm_x_kernel(tc, x, wT, us, ts, wt, offs, poffs, out):
         def load_x(j):
             nc.sync.dma_start(x_rows[j][:], x[block(j), :])
 
-        nc.sync.dma_start(neg_list[:], offs)
-        nc.sync.dma_start(pos_list[:], poffs)
         load_plane(0)
-        load_plane(1)
+        nc.sync.dma_start(row_factors[LAST - 1:LAST, :], us.rearrange("r o -> o r"))
+        nc.sync.dma_start(row_factors[LAST:P, :], wt.rearrange("r o -> o r"))
         load_x(0)
         load_x(1)
+        load_plane(1)
         load_plane(2)
-        load_plane(3)
         load_x(2)
-        load_x(3)
-        nc.scalar.dma_start(ts_table[LAST:P, :], ts[0:1, :])
-        nc.scalar.dma_start(row_factors[LAST - 1:LAST, :], us.rearrange("r o -> o r"))
-        nc.scalar.dma_start(row_factors[LAST:P, :], wt.rearrange("r o -> o r"))
         nc.vector.memset(ts_table[0:LAST, :], 0.0)
         make_identity(nc, ident[:])
         nc.gpsimd.memset(row_factors[0:LAST - 1, :], 0.0)
+
+        x_bf = [shared.tile([P, FEATURES], BF16, name=f"x_bf{j}", offset=(2, 8, 10, 11)[j] * ROOM // 2, align_bytes=MX_ALIGN) for j in range(TILES)]
+        x_grouped = [keep.tile([P, HALF, PACK], BF16, name="x_grouped", tag=f"x_grouped{h}", align_bytes=MX_ALIGN) for h in range(2)]
+        x_codes = keep.tile([P, ROWS], U32, name="x_codes", align_bytes=MX_ALIGN)
+        x_scales = keep.tile([P, ROWS], U8, name="x_scales", align_bytes=MX_ALIGN)
+
+        def round_x(j):
+            nc.gpsimd.tensor_scalar(
+                x_bf[j][:].rearrange("r (u p e) -> r u p e", u=2, e=2),
+                x_rows[j][:].rearrange("r (p u e) -> r u p e", u=2, e=2),
+                1.0, 0.0, ALU.mult, ALU.add,
+            )
+
+        def quantise_x(h, number):
+            bank = bank_tile(number)
+            for a in range(2):
+                words = x_bf[2 * h + a][:].bitcast(F32)
+                for u in range(2):
+                    nc.tensor.transpose(bank[:, block(2 * a + u)], words[:, block(u)], ident[:])
+            nc.scalar.copy(
+                flat(x_grouped[h][:]).bitcast(F32).rearrange("p (a r u) -> p a r u", a=2, u=2),
+                bank[:].rearrange("p (a u r) -> p a r u", a=2, u=2),
+            )
+            nc.vector.quantize_mx(out=x_codes[:, half(h)].bitcast(E4M3), scales=x_scales[:, half(h)], in_=flat(x_grouped[h][:]))
 
         def turn_rows(rows, number):
             bank = bank_tile(number)
@@ -85,82 +113,50 @@ def tile_attend_gspos_sm_x_kernel(tc, x, wT, us, ts, wt, offs, poffs, out):
             return bank
 
         ts_neg_row = keep.tile([P, SLOTS], F32, name="ts_neg_row")
-        ts_pos_row = keep.tile([P, ROWS], F32, name="ts_pos_row")
-        nc.vector.tensor_copy(ts_neg_row[:], ts_table[:].indirect(neg_list[:]))
-        nc.vector.tensor_copy(ts_pos_row[:], ts_table[:].indirect(pos_list[:]))
-
+        ts_pos_row = shared.tile([P, ROWS], F32, name="ts_pos_row", offset=0, align_bytes=MX_ALIGN)
         ts_neg = keep.tile([P, TILES], F32, name="ts_neg")
-        ts_neg_spread = keep.tile([P, SLOTS], F32, name="ts_neg_spread")
+        ts_neg_spread = shared.tile([P, SLOTS], F32, name="ts_neg_spread", offset=5 * ROOM, align_bytes=MX_ALIGN)
         us_col = keep.tile([P, TILES], F32, name="us_col")
         minus_us = keep.tile([P, TILES], F32, name="minus_us")
         wt_us = keep.tile([P, TILES], F32, name="wt_us")
         minus_us_tp = keep.tile([P, TILES], F32, name="minus_us_tp")
         wt_us_tp = keep.tile([P, TILES], F32, name="wt_us_tp")
 
-        turned = turn_rows(row_factors, 0)
-        nc.scalar.copy(us_col[:], turned[:, LAST - 1::P])
-        nc.scalar.mul(minus_us[:], turned[:, LAST - 1::P], -1.0)
-        for j in range(TILES):
-            nc.scalar.mul(wt_us[:, column(j)], turned[:, column(j * P + LAST)], us_col[:, column(j)])
-        turned = turn_rows(ts_neg_row, 1)
-        nc.scalar.copy(ts_neg[:], turned[:, LAST::P])
-        turned = turn_rows(ts_pos_row, 2)
-        for j in range(TILES):
-            ts_pos = turned[:, column(j * P + LAST)]
-            nc.scalar.mul(minus_us_tp[:, column(j)], ts_pos, minus_us[:, column(j)])
-            nc.scalar.mul(wt_us_tp[:, column(j)], ts_pos, wt_us[:, column(j)])
-        turned = bank_tile(3)
-        for j in range(TILES):
-            nc.tensor.transpose(turned[:, block(j)], ts_neg[:, column(j)].to_broadcast([P, P]), ident[:])
-        nc.scalar.copy(ts_neg_spread[:], turned[:])
+        def factors():
+            nc.vector.tensor_copy(ts_neg_row[:], ts_table[:].indirect(neg_list[:]))
+            nc.vector.tensor_copy(ts_pos_row[:], ts_table[:].indirect(pos_list[:]))
+            turned = turn_rows(row_factors, 0)
+            nc.vector.tensor_copy(us_col[:], turned[:, LAST - 1::P])
+            nc.vector.tensor_scalar(minus_us[:], turned[:, LAST - 1::P], -1.0, None, ALU.mult)
+            nc.vector.tensor_tensor(wt_us[:], turned[:, LAST::P], us_col[:], ALU.mult)
+            turned = turn_rows(ts_neg_row, 1)
+            nc.vector.tensor_copy(ts_neg[:], turned[:, LAST::P])
+            turned = turn_rows(ts_pos_row, 2)
+            nc.vector.tensor_tensor(minus_us_tp[:], turned[:, LAST::P], minus_us[:], ALU.mult)
+            nc.vector.tensor_tensor(wt_us_tp[:], turned[:, LAST::P], wt_us[:], ALU.mult)
+            turned = bank_tile(3)
+            for j in range(TILES):
+                nc.tensor.transpose(turned[:, block(j)], ts_neg[:, column(j)].to_broadcast([P, P]), ident[:])
+            nc.scalar.copy(ts_neg_spread[:], turned[:])
 
         w_neg = keep.tile([P, PACK, SLOTS], BF16, name="w_neg", align_bytes=MX_ALIGN)
-        w_pos = [keep.tile([P, ROWS], F32, name=f"w_pos{t}") for t in range(PACK)]
+        wd_grouped = [keep.tile([P, HALF, PACK], BF16, name="wd_grouped", tag=f"wd_grouped{h}", align_bytes=MX_ALIGN) for h in range(2)]
+        wd_codes = keep.tile([P, SLOTS], U32, name="wd_codes", align_bytes=MX_ALIGN)
+        wd_scales = keep.tile([P, SLOTS], U8, name="wd_scales", align_bytes=MX_ALIGN)
+        wi_grouped = keep.tile([P, FEATURES, PACK], BF16, name="wi_grouped", align_bytes=MX_ALIGN)
+        wi_codes = keep.tile([P, FEATURES], U32, name="wi_codes", align_bytes=MX_ALIGN)
+        wi_scales = keep.tile([P, FEATURES], U8, name="wi_scales", align_bytes=MX_ALIGN)
 
         def gather_neg(t, first, count):
             offsets = neg_list[:, first // LIST_ROWS:(first + count) // LIST_ROWS]
             nc.vector.tensor_copy(w_neg[:, t, first:first + count], planes[t][:].indirect(offsets))
 
-        def gather_pos(t):
-            nc.vector.tensor_copy(w_pos[t][:], planes[t][:].indirect(pos_list[:]))
-
-        wd_codes = keep.tile([P, SLOTS], U32, name="wd_codes", align_bytes=MX_ALIGN)
-        wd_scales = keep.tile([P, SLOTS], U8, name="wd_scales", align_bytes=MX_ALIGN)
-        x_bf = [keep.tile([P, FEATURES], BF16, name=f"x_bf{j}", align_bytes=MX_ALIGN) for j in range(TILES)]
-        x_codes = keep.tile([P, ROWS], U32, name="x_codes", align_bytes=MX_ALIGN)
-        x_scales = keep.tile([P, ROWS], U8, name="x_scales", align_bytes=MX_ALIGN)
-
-        def quantise_neg_along_d(h):
-            slots = slice(h * HALF, (h + 1) * HALF)
-            grouped = keep.tile([P, HALF, PACK], BF16, name="wd_grouped", tag=f"wd_grouped{h}", align_bytes=MX_ALIGN)
-            nc.scalar.copy(
-                grouped[:].rearrange("p (c i) t -> p c t i", i=RUN),
-                w_neg[:, :, slots].rearrange("p t (c i) -> p c t i", i=RUN),
+        def quantise_neg_along_d(h, copy):
+            copy(
+                wd_grouped[h][:].rearrange("p (c i) t -> p c t i", i=RUN),
+                w_neg[:, :, half(h)].rearrange("p t (c i) -> p c t i", i=RUN),
             )
-            nc.vector.quantize_mx(out=wd_codes[:, slots].bitcast(E4M3), scales=wd_scales[:, slots], in_=flat(grouped[:]))
-
-        def quantise_x(h, number):
-            for j in (2 * h, 2 * h + 1):
-                nc.gpsimd.tensor_scalar(
-                    x_bf[j][:].rearrange("r (u p e) -> r u p e", u=2, e=2),
-                    x_rows[j][:].rearrange("r (p u e) -> r u p e", u=2, e=2),
-                    1.0, 0.0, ALU.mult, ALU.add,
-                )
-            bank = bank_tile(number)
-            for a in range(2):
-                words = x_bf[2 * h + a][:].bitcast(F32)
-                for u in range(2):
-                    nc.tensor.transpose(bank[:, block(2 * a + u)], words[:, block(u)], ident[:])
-            rows = slice(h * HALF, (h + 1) * HALF)
-            grouped = keep.tile([P, HALF, PACK], BF16, name="x_grouped", tag=f"x_grouped{h}", align_bytes=MX_ALIGN)
-            nc.scalar.copy(
-                flat(grouped[:]).bitcast(F32).rearrange("p (a r u) -> p a r u", a=2, u=2),
-                bank[:].rearrange("p (a u r) -> p a r u", a=2, u=2),
-            )
-            nc.vector.quantize_mx(out=x_codes[:, rows].bitcast(E4M3), scales=x_scales[:, rows], in_=flat(grouped[:]))
-
-        wi_grouped = keep.tile([P, FEATURES, PACK], BF16, name="wi_grouped", align_bytes=MX_ALIGN)
-        wi_scales = keep.tile([P, FEATURES], U8, name="wi_scales", align_bytes=MX_ALIGN)
+            nc.vector.quantize_mx(out=wd_codes[:, half(h)].bitcast(E4M3), scales=wd_scales[:, half(h)], in_=flat(wd_grouped[h][:]))
 
         def turn_neg(m, number):
             words = w_neg[:].rearrange("p t i -> p (t i)").bitcast(F32).rearrange("p (t w) -> p t w", t=PACK)
@@ -174,70 +170,68 @@ def tile_attend_gspos_sm_x_kernel(tc, x, wT, us, ts, wt, offs, poffs, out):
         def quantise_neg_along_i():
             nc.vector.quantize_mx(out=wi_codes[:].bitcast(E4M3), scales=wi_scales[:], in_=flat(wi_grouped[:]))
 
-        minus_z = [keep.tile([P, SLOTS + 1], F32, name=f"minus_z{j}", tag=f"minus_z{j}", align_bytes=MX_ALIGN) for j in range(TILES)]
-        e = keep.tile([P, TILES, SLOTS + 8], F32, name="e")
+        w_pos = [keep.tile([P, ROWS], F32, name=f"w_pos{t}") for t in range(PACK)]
+        w_pos_rows = {}
+        minus_z = shared.tile([P, TILES, PADDED], F32, name="minus_z", offset=8 * ROOM, align_bytes=MX_ALIGN)
+        e = keep.tile([P, TILES, PADDED], F32, name="e")
         minus_m = keep.tile([P, TILES], F32, name="minus_m")
         tot = keep.tile([P, TILES], F32, name="tot")
         inv = keep.tile([P, TILES], F32, name="inv")
         pos_share = keep.tile([P, TILES], F32, name="pos_share")
-        scaled_T = [keep.tile([P, TILES, HALF], F32, name=f"scaled_T{r}") for r in range(2)]
-        pos_banks = {}
-        w_pos_rows = {}
 
-        def spent(tag, count):
-            return keep.tile([P, count, FEATURES], F32, name="products", tag=tag, align_bytes=MX_ALIGN)
+        def gather_pos(t):
+            nc.scalar.activation(w_pos[t][:], planes[t][:].indirect(pos_list[:]), ACT.Copy)
+
+        def turn_pos(t):
+            for j in range(TILES):
+                nc.tensor.transpose(pos_banks[j][:, t::PACK], w_pos[t][:, block(j)], ident[:])
 
         def positive_score(j, products):
-            bank = bank_tile(TILES + j)
-            for t in (2, 0, 1, 3):
-                nc.tensor.transpose(bank[:, t::PACK], w_pos[t][:, block(j)], ident[:])
-            pos_banks[j] = bank
             nc.vector.scalar_tensor_tensor(
-                products, bank[:], minus_us_tp[:, column(j)], x_rows[j][:], ALU.mult, ALU.mult,
-                accum_out=minus_z[j][:, column(SLOTS)],
+                products, pos_banks[j][:], minus_us_tp[:, column(j)], x_rows[j][:], ALU.mult, ALU.mult,
+                accum_out=minus_z[:, j, column(SLOTS)],
             )
 
-        def keep_positives(j, tag):
-            w_pos_rows[j] = keep.tile([P, FEATURES], F32, name="w_pos_rows", tag=tag, align_bytes=MX_ALIGN)
+        def keep_positives(j):
+            w_pos_rows[j] = shared.tile([P, FEATURES], F32, name=f"w_pos_rows{j}", offset=(8 + j) * ROOM, align_bytes=MX_ALIGN)
             nc.scalar.mul(w_pos_rows[j][:], pos_banks[j][:], wt_us_tp[:, column(j)])
+
+        scaled = [keep.tile([P, TILES, HALF], F32, name=f"scaled{r}") for r in range(2)]
+
+        def scores(h, rows, number):
+            bank = bank_tile(number)
+            for n in range(2):
+                slots = block(2 * h + n)
+                nc.tensor.matmul_mx(
+                    out=bank[:, half(n)], lhsT=wd_codes[:, slots].bitcast(E4M3), lhsT_scale=wd_scales[:, slots],
+                    rhs=x_codes[:, half(rows)].bitcast(E4M3), rhs_scale=x_scales[:, half(rows)], start=True, stop=True,
+                )
+            for n in range(2):
+                s = 2 * h + n
+                nc.scalar.activation(scaled[rows][:, s, :], bank[:, half(n)], ACT.Copy, scale=ts_neg[:, column(s)])
+
+        def softmax(j, number):
+            bank = bank_tile(number)
+            for s in range(TILES):
+                nc.tensor.transpose(bank[:, block(s)], scaled[j // 2][:, s, block(j % 2)], ident[:])
+            nc.vector.tensor_scalar(
+                minus_z[:, j, 0:SLOTS], bank[:], minus_us[:, column(j)], minus_z[:, j, column(SLOTS)], ALU.mult, ALU.min,
+                accum_out=minus_m[:, column(j)],
+            )
+            nc.scalar.activation(
+                e[:, j, 0:SLOTS + 1], minus_z[:, j, 0:SLOTS + 1], ACT.Exp, bias=minus_m[:, column(j)], scale=-1.0,
+                accum_out=tot[:, column(j)],
+            )
+
+        def row_factor(j):
+            nc.vector.reciprocal(inv[:, column(j)], tot[:, column(j)])
 
         def positive_share(j):
             nc.scalar.activation(
                 pos_share[:, column(j)], e[:, j, column(SLOTS)], ACT.Identity, scale=inv[:, column(j)], bias=-1.0
             )
 
-        def scores_by_slot(h, rows, number):
-            a_T = bank_tile(number)
-            for n in range(2):
-                slots = block(2 * h + n)
-                nc.tensor.matmul_mx(
-                    out=a_T[:, n * HALF:(n + 1) * HALF], lhsT=wd_codes[:, slots].bitcast(E4M3), lhsT_scale=wd_scales[:, slots],
-                    rhs=x_codes[:, rows * HALF:(rows + 1) * HALF].bitcast(E4M3), rhs_scale=x_scales[:, rows * HALF:(rows + 1) * HALF], start=True, stop=True,
-                )
-            for n in range(2):
-                s = 2 * h + n
-                nc.scalar.activation(scaled_T[rows][:, s, :], a_T[:, n * HALF:(n + 1) * HALF], ACT.Copy, scale=ts_neg[:, column(s)])
-
-        def exponentials(j):
-            nc.scalar.activation(
-                e[:, j, 0:SLOTS + 1], minus_z[j][:], ACT.Exp, bias=minus_m[:, column(j)], scale=-1.0,
-                accum_out=tot[:, column(j)],
-            )
-
-        def softmax_by_slot(j, number):
-            scaled = bank_tile(number)
-            for s in range(TILES):
-                nc.tensor.transpose(scaled[:, block(s)], scaled_T[j // 2][:, s, block(j % 2)], ident[:])
-            nc.vector.tensor_scalar(
-                minus_z[j][:, 0:SLOTS], scaled[:], minus_us[:, column(j)], minus_z[j][:, column(SLOTS)], ALU.mult, ALU.min,
-                accum_out=minus_m[:, column(j)],
-            )
-            exponentials(j)
-
-        def row_factor(j):
-            nc.vector.reciprocal(inv[:, column(j)], tot[:, column(j)])
-
-        g = [keep.tile([P, SLOTS], BF16, name="g", tag=f"g{j}", align_bytes=MX_ALIGN) for j in range(TILES)]
+        g = [keep.tile([P, SLOTS], BF16, name=f"g{j}", align_bytes=MX_ALIGN) for j in range(TILES)]
         g_grouped = [keep.tile([P, P, PACK], BF16, name=f"g_grouped{j}", align_bytes=MX_ALIGN) for j in range(TILES)]
         g_codes = [keep.tile([P, P], U32, name=f"g_codes{j}", align_bytes=MX_ALIGN) for j in range(TILES)]
         g_scales = [keep.tile([P, P], U8, name=f"g_scales{j}", align_bytes=MX_ALIGN) for j in range(TILES)]
@@ -274,53 +268,57 @@ def tile_attend_gspos_sm_x_kernel(tc, x, wT, us, ts, wt, offs, poffs, out):
                 )
                 nc.sync.dma_start(out[block(j), cols], result[j][:, cols])
 
+        factors()
+        round_x(0)
+        round_x(1)
+        quantise_x(0, 1)
+        wt_us_ts = keep.tile([P, TILES, SLOTS], F32, name="wt_us_ts")
+        for j in range(TILES):
+            nc.gpsimd.tensor_scalar(wt_us_ts[:, j, :], ts_neg_spread[:], wt_us[:, column(j)], 0.0, ALU.mult, ALU.add)
+        last = PACK - 1
+        planes.append(shared.tile([P, ITEMS], F32, name="last_plane", offset=0, align_bytes=MX_ALIGN))
+        x_rows.append(shared.tile([P, FEATURES], F32, name="last_x", offset=4 * ROOM, align_bytes=MX_ALIGN))
+        load_plane(last)
+        load_x(TILES - 1)
+        round_x(2)
+        round_x(3)
+        pos_banks = [bank_tile(TILES + j) for j in range(TILES)]
         for t in range(PACK - 1):
-            if t == 0:
-                rounded_plane = keep.tile([P, ITEMS], BF16, name="rounded_plane")
-                nc.scalar.activation(rounded_plane[:], planes[t][:], ACT.Copy)
-                nc.scalar.activation(w_neg[:, t, :], rounded_plane[:].indirect(neg_list[:]), ACT.Copy)
-            else:
-                gather_neg(t, 0, SLOTS)
+            gather_neg(t, 0, SLOTS)
             gather_pos(t)
             if t == 1:
                 turn_neg(0, 0)
-        gather_neg(PACK - 1, 0, HALF)
-        gather_neg(PACK - 1, HALF, HALF)
-        quantise_x(0, 1)
-        quantise_neg_along_d(0)
-        quantise_neg_along_d(1)
-        gather_pos(PACK - 1)
-        quantise_x(1, 7)
-
-        behind_first_half = spent("wd_grouped0", 1)
-        behind_second_half = spent("wd_grouped1", 3)
-        wt_us_ts = keep.tile([P, TILES, SLOTS], F32, name="wt_us_ts", tag="x_grouped1", align_bytes=MX_ALIGN)
-        for j in range(TILES):
-            nc.gpsimd.tensor_scalar(wt_us_ts[:, j, :], ts_neg_spread[:], wt_us[:, column(j)], 0.0, ALU.mult, ALU.add)
-        banks = (0, 1, 3, 2)
-        scores_by_slot(0, 0, banks[0])
-        scores_by_slot(1, 0, banks[1])
-        scores_by_slot(0, 1, banks[2])
-        scores_by_slot(1, 1, banks[3])
+            turn_pos(t)
+        gather_neg(last, 0, HALF)
+        gather_neg(last, HALF, HALF)
+        gather_pos(last)
+        quantise_neg_along_d(0, nc.vector.tensor_copy)
+        quantise_neg_along_d(1, nc.scalar.copy)
+        turn_pos(last)
+        quantise_x(1, 3)
+        behind_first_half = keep.tile([P, 1, FEATURES], F32, name="products", tag="wd_grouped0", align_bytes=MX_ALIGN)
+        behind_second_half = keep.tile([P, 3, FEATURES], F32, name="products", tag="wd_grouped1", align_bytes=MX_ALIGN)
+        scores(0, 0, 0)
+        scores(1, 0, 1)
+        scores(0, 1, 2)
+        scores(1, 1, 3)
         positive_score(0, behind_first_half[:, 0, :])
-        positive_score(1, behind_second_half[:, 0, :])
-        positive_score(2, behind_second_half[:, 1, :])
-        positive_score(3, behind_second_half[:, 2, :])
+        for j in range(1, TILES):
+            positive_score(j, behind_second_half[:, j - 1, :])
         for j in range(TILES):
-            softmax_by_slot(j, banks[j])
+            softmax(j, j)
             if j >= 2:
                 row_factor(j - 2)
-        turn_neg(1, banks[3])
+        turn_neg(1, 3)
         for j in range(TILES):
-            gradient(j, banks[j])
+            gradient(j, j)
             if j < 2:
                 row_factor(j + 2)
-        wi_codes = keep.tile([P, FEATURES], U32, name="wi_codes", tag="x_grouped1", align_bytes=MX_ALIGN)
         quantise_neg_along_i()
-        for j, tag in enumerate(("w_pos_rows", "minus_z3", "g1", "g3")):
-            keep_positives(j, tag)
-            positive_share(j)
         for j in range(TILES):
-            multiply(j, banks[j])
+            positive_share(j)
+            keep_positives(j)
+        for j in range(TILES):
+            multiply(j, j)
         for j in range(TILES):
             finish(j, 2 if j == TILES - 1 else 1)

@@ -140,7 +140,7 @@ def tile_attend_gspos_sm_x_kernel(tc, x, wT, us, ts, wt, offs, poffs, out):
             nc.scalar.copy(ts_neg_spread[:], turned[:])
 
         w_neg = keep.tile([P, PACK, SLOTS], BF16, name="w_neg", align_bytes=MX_ALIGN)
-        wd_grouped = [keep.tile([P, HALF, PACK], BF16, name="wd_grouped", tag=f"wd_grouped{h}", align_bytes=MX_ALIGN) for h in range(2)]
+        wd_grouped = keep.tile([P, SLOTS, PACK], BF16, name="wd_grouped", align_bytes=MX_ALIGN)
         wd_codes = keep.tile([P, SLOTS], U32, name="wd_codes", align_bytes=MX_ALIGN)
         wd_scales = keep.tile([P, SLOTS], U8, name="wd_scales", align_bytes=MX_ALIGN)
         wi_grouped = keep.tile([P, FEATURES, PACK], BF16, name="wi_grouped", align_bytes=MX_ALIGN)
@@ -149,14 +149,18 @@ def tile_attend_gspos_sm_x_kernel(tc, x, wT, us, ts, wt, offs, poffs, out):
 
         def gather_neg(t, first, count):
             offsets = neg_list[:, first // LIST_ROWS:(first + count) // LIST_ROWS]
-            nc.vector.tensor_copy(w_neg[:, t, first:first + count], planes[t][:].indirect(offsets))
+            slots = slice(first, first + count)
+            target = wd_grouped[:, slots, t] if t == PACK - 1 else w_neg[:, t, slots]
+            nc.vector.tensor_copy(target, planes[t][:].indirect(offsets))
 
-        def quantise_neg_along_d(h, copy):
-            copy(
-                wd_grouped[h][:].rearrange("p (c i) t -> p c t i", i=RUN),
-                w_neg[:, :, half(h)].rearrange("p t (c i) -> p c t i", i=RUN),
+        def group_early_planes():
+            nc.vector.tensor_copy(
+                wd_grouped[:, :, 0:PACK - 1].rearrange("p (c i) t -> p c t i", i=RUN),
+                w_neg[:, 0:PACK - 1, :].rearrange("p t (c i) -> p c t i", i=RUN),
             )
-            nc.vector.quantize_mx(out=wd_codes[:, half(h)].bitcast(E4M3), scales=wd_scales[:, half(h)], in_=flat(wd_grouped[h][:]))
+
+        def quantise_neg_along_d(h):
+            nc.vector.quantize_mx(out=wd_codes[:, half(h)].bitcast(E4M3), scales=wd_scales[:, half(h)], in_=flat(wd_grouped[:, half(h), :]))
 
         def turn_neg(m, number):
             words = w_neg[:].rearrange("p t i -> p (t i)").bitcast(F32).rearrange("p (t w) -> p t w", t=PACK)
@@ -289,22 +293,23 @@ def tile_attend_gspos_sm_x_kernel(tc, x, wT, us, ts, wt, offs, poffs, out):
             if t == 1:
                 turn_neg(0, 0)
             turn_pos(t)
+        group_early_planes()
         gather_neg(last, 0, HALF)
         gather_neg(last, HALF, HALF)
         gather_pos(last)
-        quantise_neg_along_d(0, nc.vector.tensor_copy)
-        quantise_neg_along_d(1, nc.scalar.copy)
+        quantise_neg_along_d(0)
+        quantise_neg_along_d(1)
         turn_pos(last)
         quantise_x(1, 3)
-        behind_first_half = keep.tile([P, 1, FEATURES], F32, name="products", tag="wd_grouped0", align_bytes=MX_ALIGN)
-        behind_second_half = keep.tile([P, 3, FEATURES], F32, name="products", tag="wd_grouped1", align_bytes=MX_ALIGN)
+        behind_first_half = keep.tile([P, 2, FEATURES], F32, name="products")
+        behind_second_half = keep.tile([P, 2, FEATURES], F32, name="products", tag="x_grouped1", align_bytes=MX_ALIGN)
         scores(0, 0, 0)
         scores(1, 0, 1)
         scores(0, 1, 2)
         scores(1, 1, 3)
-        positive_score(0, behind_first_half[:, 0, :])
-        for j in range(1, TILES):
-            positive_score(j, behind_second_half[:, j - 1, :])
+        for j in range(TILES):
+            positive_score(j, (behind_first_half, behind_second_half)[j // 2][:, j % 2, :])
+        nc.scalar.copy(w_neg[:, last, :], wd_grouped[:, :, last])
         for j in range(TILES):
             softmax(j, j)
             if j >= 2:

@@ -139,7 +139,7 @@ def tile_attend_gspos_sm_x_kernel(tc, x, wT, us, ts, wt, offs, poffs, out):
                 nc.tensor.transpose(turned[:, block(j)], ts_neg[:, column(j)].to_broadcast([P, P]), ident[:])
             nc.scalar.copy(ts_neg_spread[:], turned[:])
 
-        w_neg = keep.tile([P, PACK, SLOTS], BF16, name="w_neg", align_bytes=MX_ALIGN)
+        w_neg = keep.tile([P, PACK - 1, SLOTS], BF16, name="w_neg", align_bytes=MX_ALIGN)
         wd_grouped = keep.tile([P, SLOTS, PACK], BF16, name="wd_grouped", align_bytes=MX_ALIGN)
         wd_codes = keep.tile([P, SLOTS], U32, name="wd_codes", align_bytes=MX_ALIGN)
         wd_scales = keep.tile([P, SLOTS], U8, name="wd_scales", align_bytes=MX_ALIGN)
@@ -156,19 +156,21 @@ def tile_attend_gspos_sm_x_kernel(tc, x, wT, us, ts, wt, offs, poffs, out):
         def group_early_planes():
             nc.vector.tensor_copy(
                 wd_grouped[:, :, 0:PACK - 1].rearrange("p (c i) t -> p c t i", i=RUN),
-                w_neg[:, 0:PACK - 1, :].rearrange("p t (c i) -> p c t i", i=RUN),
+                w_neg[:].rearrange("p t (c i) -> p c t i", i=RUN),
             )
 
         def quantise_neg_along_d(h):
             nc.vector.quantize_mx(out=wd_codes[:, half(h)].bitcast(E4M3), scales=wd_scales[:, half(h)], in_=flat(wd_grouped[:, half(h), :]))
 
+        late = []
+
         def turn_neg(m, number):
-            words = w_neg[:].rearrange("p t i -> p (t i)").bitcast(F32).rearrange("p (t w) -> p t w", t=PACK)
+            words = [w_neg[:, t, :].bitcast(F32) for t in range(PACK - 1)] + [last_neg[:].bitcast(F32) for last_neg in late]
             wi_words = flat(wi_grouped[:]).bitcast(F32).rearrange("s (p t u) -> s p t u", t=PACK, u=2)
             bank = bank_tile(number)
             for a in reversed(range(2)):
                 for u in range(2):
-                    nc.tensor.transpose(bank[:, block(2 * a + u)], words[:, 2 * m + a, u::2], ident[:])
+                    nc.tensor.transpose(bank[:, block(2 * a + u)], words[2 * m + a][:, u::2], ident[:])
             nc.scalar.copy(wi_words[:, :, 2 * m:2 * m + 2, :], bank[:].rearrange("s (a u p) -> s p a u", a=2, u=2))
 
         def quantise_neg_along_i():
@@ -301,7 +303,7 @@ def tile_attend_gspos_sm_x_kernel(tc, x, wT, us, ts, wt, offs, poffs, out):
         quantise_neg_along_d(1)
         turn_pos(last)
         quantise_x(1, 3)
-        behind_first_half = keep.tile([P, 2, FEATURES], F32, name="products")
+        behind_first_half = keep.tile([P, 2, FEATURES], F32, name="products", tag="products", align_bytes=MX_ALIGN)
         behind_second_half = keep.tile([P, 2, FEATURES], F32, name="products", tag="x_grouped1", align_bytes=MX_ALIGN)
         scores(0, 0, 0)
         scores(1, 0, 1)
@@ -309,7 +311,8 @@ def tile_attend_gspos_sm_x_kernel(tc, x, wT, us, ts, wt, offs, poffs, out):
         scores(1, 1, 3)
         for j in range(TILES):
             positive_score(j, (behind_first_half, behind_second_half)[j // 2][:, j % 2, :])
-        nc.scalar.copy(w_neg[:, last, :], wd_grouped[:, :, last])
+        late.append(keep.tile([P, SLOTS], BF16, name="last_neg", tag="x_grouped1", align_bytes=MX_ALIGN))
+        nc.gpsimd.tensor_scalar(late[0][:], wd_grouped[:, :, last], 1.0, 0.0, ALU.mult, ALU.add)
         for j in range(TILES):
             softmax(j, j)
             if j >= 2:

@@ -26,7 +26,14 @@ LIST_ROWS = 16
 MX_ALIGN = 64
 ROOM = 2048
 RUN = 4
+ROUNDED_ON_SCALAR = 2
 PADDED = SLOTS + 8
+
+LAST_PLANE_AT = 0
+TS_POS_AT = 0
+FIRST_PLANE_AT = 4 * ROOM
+X_AT = FIRST_PLANE_AT + 2 * ROOM
+MINUS_Z_AT = 12 * ROOM
 
 
 def tile_attend_gspos_sm_x_kernel(tc, x, wT, us, ts, wt, offs, poffs, out):
@@ -55,8 +62,16 @@ def tile_attend_gspos_sm_x_kernel(tc, x, wT, us, ts, wt, offs, poffs, out):
         pos_list = keep.tile([P, ROWS // LIST_ROWS], U16, name="pos_list")
         ts_table = keep.tile([P, ITEMS], F32, name="ts_table")
         row_factors = keep.tile([P, ROWS], F32, name="row_factors")
-        planes = [keep.tile([P, ITEMS], F32, name=f"plane{t}") for t in range(PACK - 1)]
-        x_rows = [keep.tile([P, FEATURES], F32, name=f"x_rows{j}") for j in range(TILES - 1)]
+        planes = [
+            shared.tile([P, ITEMS], F32, name="plane0", offset=FIRST_PLANE_AT, align_bytes=MX_ALIGN),
+            shared.tile([P, ITEMS], F32, name="plane1", offset=FIRST_PLANE_AT + 4 * ROOM, align_bytes=MX_ALIGN),
+            keep.tile([P, ITEMS], F32, name="plane2"),
+            shared.tile([P, ITEMS], F32, name="plane3", offset=LAST_PLANE_AT, align_bytes=MX_ALIGN),
+        ]
+        x_rows = [
+            shared.tile([P, FEATURES], F32, name=f"x_rows{j}", offset=X_AT + j * ROOM, align_bytes=MX_ALIGN)
+            for j in range(TILES)
+        ]
         ident = keep.tile([P, P], F32, name="ident")
 
         wT_planes = wT.rearrange("(p t) c -> t p c", t=PACK)
@@ -73,26 +88,27 @@ def tile_attend_gspos_sm_x_kernel(tc, x, wT, us, ts, wt, offs, poffs, out):
         load_plane(0)
         nc.sync.dma_start(row_factors[LAST - 1:LAST, :], us.rearrange("r o -> o r"))
         nc.sync.dma_start(row_factors[LAST:P, :], wt.rearrange("r o -> o r"))
-        load_x(0)
-        load_x(1)
         load_plane(1)
         load_plane(2)
-        load_x(2)
         nc.vector.memset(ts_table[0:LAST, :], 0.0)
         make_identity(nc, ident[:])
         nc.gpsimd.memset(row_factors[0:LAST - 1, :], 0.0)
 
-        x_bf = [shared.tile([P, FEATURES], BF16, name=f"x_bf{j}", offset=(2, 8, 10, 11)[j] * ROOM // 2, align_bytes=MX_ALIGN) for j in range(TILES)]
-        x_grouped = [keep.tile([P, HALF, PACK], BF16, name="x_grouped", tag=f"x_grouped{h}", align_bytes=MX_ALIGN) for h in range(2)]
+        x_bf = [keep.tile([P, FEATURES], BF16, name=f"x_bf{j}", align_bytes=MX_ALIGN) for j in range(TILES)]
+        x_grouped = [
+            keep.tile([P, HALF, PACK], BF16, name="x_grouped", tag=f"x_grouped{h}", align_bytes=MX_ALIGN)
+            for h in range(2)
+        ]
         x_codes = keep.tile([P, ROWS], U32, name="x_codes", align_bytes=MX_ALIGN)
         x_scales = keep.tile([P, ROWS], U8, name="x_scales", align_bytes=MX_ALIGN)
 
         def round_x(j):
-            nc.gpsimd.tensor_scalar(
-                x_bf[j][:].rearrange("r (u p e) -> r u p e", u=2, e=2),
-                x_rows[j][:].rearrange("r (p u e) -> r u p e", u=2, e=2),
-                1.0, 0.0, ALU.mult, ALU.add,
-            )
+            rounded = x_bf[j][:].rearrange("r (u p e) -> r u p e", u=2, e=2)
+            rows = x_rows[j][:].rearrange("r (p u e) -> r u p e", u=2, e=2)
+            if j == ROUNDED_ON_SCALAR:
+                nc.scalar.activation(rounded, rows, ACT.Copy)
+            else:
+                nc.gpsimd.tensor_scalar(rounded, rows, 1.0, 0.0, ALU.mult, ALU.add)
 
         def quantise_x(h, number):
             bank = bank_tile(number)
@@ -113,9 +129,9 @@ def tile_attend_gspos_sm_x_kernel(tc, x, wT, us, ts, wt, offs, poffs, out):
             return bank
 
         ts_neg_row = keep.tile([P, SLOTS], F32, name="ts_neg_row")
-        ts_pos_row = shared.tile([P, ROWS], F32, name="ts_pos_row", offset=0, align_bytes=MX_ALIGN)
+        ts_pos_row = shared.tile([P, ROWS], F32, name="ts_pos_row", offset=TS_POS_AT, align_bytes=MX_ALIGN)
         ts_neg = keep.tile([P, TILES], F32, name="ts_neg")
-        ts_neg_spread = shared.tile([P, SLOTS], F32, name="ts_neg_spread", offset=5 * ROOM, align_bytes=MX_ALIGN)
+        ts_neg_spread = keep.tile([P, SLOTS], F32, name="ts_neg_spread")
         us_col = keep.tile([P, TILES], F32, name="us_col")
         minus_us = keep.tile([P, TILES], F32, name="minus_us")
         wt_us = keep.tile([P, TILES], F32, name="wt_us")
@@ -140,6 +156,7 @@ def tile_attend_gspos_sm_x_kernel(tc, x, wT, us, ts, wt, offs, poffs, out):
             nc.scalar.copy(ts_neg_spread[:], turned[:])
 
         w_neg = keep.tile([P, PACK - 1, SLOTS], BF16, name="w_neg", align_bytes=MX_ALIGN)
+        neg_planes = [w_neg[:, t, :] for t in range(PACK - 1)]
         wd_grouped = keep.tile([P, SLOTS, PACK], BF16, name="wd_grouped", align_bytes=MX_ALIGN)
         wd_codes = keep.tile([P, SLOTS], U32, name="wd_codes", align_bytes=MX_ALIGN)
         wd_scales = keep.tile([P, SLOTS], U8, name="wd_scales", align_bytes=MX_ALIGN)
@@ -147,11 +164,9 @@ def tile_attend_gspos_sm_x_kernel(tc, x, wT, us, ts, wt, offs, poffs, out):
         wi_codes = keep.tile([P, FEATURES], U32, name="wi_codes", align_bytes=MX_ALIGN)
         wi_scales = keep.tile([P, FEATURES], U8, name="wi_scales", align_bytes=MX_ALIGN)
 
-        def gather_neg(t, first, count):
-            offsets = neg_list[:, first // LIST_ROWS:(first + count) // LIST_ROWS]
-            slots = slice(first, first + count)
-            target = wd_grouped[:, slots, t] if t == PACK - 1 else w_neg[:, t, slots]
-            nc.vector.tensor_copy(target, planes[t][:].indirect(offsets))
+        def gather_neg(t):
+            target = wd_grouped[:, :, t] if t == PACK - 1 else w_neg[:, t, :]
+            nc.vector.tensor_copy(target, planes[t][:].indirect(neg_list[:]))
 
         def group_early_planes():
             nc.vector.tensor_copy(
@@ -159,18 +174,15 @@ def tile_attend_gspos_sm_x_kernel(tc, x, wT, us, ts, wt, offs, poffs, out):
                 w_neg[:].rearrange("p t (c i) -> p c t i", i=RUN),
             )
 
-        def quantise_neg_along_d(h):
-            nc.vector.quantize_mx(out=wd_codes[:, half(h)].bitcast(E4M3), scales=wd_scales[:, half(h)], in_=flat(wd_grouped[:, half(h), :]))
-
-        late = []
+        def quantise_neg_along_d():
+            nc.vector.quantize_mx(out=wd_codes[:].bitcast(E4M3), scales=wd_scales[:], in_=flat(wd_grouped[:]))
 
         def turn_neg(m, number):
-            words = [w_neg[:, t, :].bitcast(F32) for t in range(PACK - 1)] + [last_neg[:].bitcast(F32) for last_neg in late]
             wi_words = flat(wi_grouped[:]).bitcast(F32).rearrange("s (p t u) -> s p t u", t=PACK, u=2)
             bank = bank_tile(number)
             for a in reversed(range(2)):
                 for u in range(2):
-                    nc.tensor.transpose(bank[:, block(2 * a + u)], words[2 * m + a][:, u::2], ident[:])
+                    nc.tensor.transpose(bank[:, block(2 * a + u)], neg_planes[2 * m + a].bitcast(F32)[:, u::2], ident[:])
             nc.scalar.copy(wi_words[:, :, 2 * m:2 * m + 2, :], bank[:].rearrange("s (a u p) -> s p a u", a=2, u=2))
 
         def quantise_neg_along_i():
@@ -178,7 +190,7 @@ def tile_attend_gspos_sm_x_kernel(tc, x, wT, us, ts, wt, offs, poffs, out):
 
         w_pos = [keep.tile([P, ROWS], F32, name=f"w_pos{t}") for t in range(PACK)]
         w_pos_rows = {}
-        minus_z = shared.tile([P, TILES, PADDED], F32, name="minus_z", offset=8 * ROOM, align_bytes=MX_ALIGN)
+        minus_z = shared.tile([P, TILES, PADDED], F32, name="minus_z", offset=MINUS_Z_AT, align_bytes=MX_ALIGN)
         e = keep.tile([P, TILES, PADDED], F32, name="e")
         minus_m = keep.tile([P, TILES], F32, name="minus_m")
         tot = keep.tile([P, TILES], F32, name="tot")
@@ -199,7 +211,9 @@ def tile_attend_gspos_sm_x_kernel(tc, x, wT, us, ts, wt, offs, poffs, out):
             )
 
         def keep_positives(j):
-            w_pos_rows[j] = shared.tile([P, FEATURES], F32, name=f"w_pos_rows{j}", offset=(8 + j) * ROOM, align_bytes=MX_ALIGN)
+            w_pos_rows[j] = shared.tile(
+                [P, FEATURES], F32, name=f"w_pos_rows{j}", offset=MINUS_Z_AT + j * ROOM, align_bytes=MX_ALIGN
+            )
             nc.scalar.mul(w_pos_rows[j][:], pos_banks[j][:], wt_us_tp[:, column(j)])
 
         scaled = [keep.tile([P, TILES, HALF], F32, name=f"scaled{r}") for r in range(2)]
@@ -274,52 +288,53 @@ def tile_attend_gspos_sm_x_kernel(tc, x, wT, us, ts, wt, offs, poffs, out):
                 )
                 nc.sync.dma_start(out[block(j), cols], result[j][:, cols])
 
+        def bank_of(j):
+            return (j + 3) % TILES
+
+        last = PACK - 1
         factors()
-        round_x(0)
-        round_x(1)
-        quantise_x(0, 1)
+        load_plane(last)
         wt_us_ts = keep.tile([P, TILES, SLOTS], F32, name="wt_us_ts")
         for j in range(TILES):
             nc.gpsimd.tensor_scalar(wt_us_ts[:, j, :], ts_neg_spread[:], wt_us[:, column(j)], 0.0, ALU.mult, ALU.add)
-        last = PACK - 1
-        planes.append(shared.tile([P, ITEMS], F32, name="last_plane", offset=0, align_bytes=MX_ALIGN))
-        x_rows.append(shared.tile([P, FEATURES], F32, name="last_x", offset=4 * ROOM, align_bytes=MX_ALIGN))
-        load_plane(last)
-        load_x(TILES - 1)
-        round_x(2)
-        round_x(3)
         pos_banks = [bank_tile(TILES + j) for j in range(TILES)]
         for t in range(PACK - 1):
-            gather_neg(t, 0, SLOTS)
+            gather_neg(t)
             gather_pos(t)
             if t == 1:
                 turn_neg(0, 0)
+                for j in range(TILES):
+                    load_x(j)
             turn_pos(t)
         group_early_planes()
-        gather_neg(last, 0, HALF)
-        gather_neg(last, HALF, HALF)
+        gather_neg(last)
         gather_pos(last)
-        quantise_neg_along_d(0)
-        quantise_neg_along_d(1)
+        quantise_neg_along_d()
         turn_pos(last)
-        quantise_x(1, 3)
-        behind_first_half = keep.tile([P, 2, FEATURES], F32, name="products", tag="products", align_bytes=MX_ALIGN)
-        behind_second_half = keep.tile([P, 2, FEATURES], F32, name="products", tag="x_grouped1", align_bytes=MX_ALIGN)
-        scores(0, 0, 0)
-        scores(1, 0, 1)
-        scores(0, 1, 2)
-        scores(1, 1, 3)
         for j in range(TILES):
-            positive_score(j, (behind_first_half, behind_second_half)[j // 2][:, j % 2, :])
-        late.append(keep.tile([P, SLOTS], BF16, name="last_neg", tag="x_grouped1", align_bytes=MX_ALIGN))
-        nc.gpsimd.tensor_scalar(late[0][:], wd_grouped[:, :, last], 1.0, 0.0, ALU.mult, ALU.add)
+            round_x(j)
+        quantise_x(0, 1)
+        quantise_x(1, 2)
+        first_products = keep.tile([P, FEATURES], F32, name="first_products")
+        second_products = keep.tile([P, FEATURES], F32, name="second_products", tag="x_grouped0", align_bytes=MX_ALIGN)
+        last_products = keep.tile([P, 2, FEATURES], F32, name="last_products", tag="x_grouped1", align_bytes=MX_ALIGN)
+        products = [first_products[:], second_products[:], last_products[:, 0, :], last_products[:, 1, :]]
+        scores(0, 0, 3)
+        scores(1, 0, 0)
+        scores(0, 1, 1)
+        scores(1, 1, 2)
         for j in range(TILES):
-            softmax(j, j)
+            positive_score(j, products[j])
+        for j in range(TILES):
+            softmax(j, bank_of(j))
             if j >= 2:
                 row_factor(j - 2)
-        turn_neg(1, 3)
+        last_neg = keep.tile([P, SLOTS], BF16, name="last_neg", tag="x_grouped1", align_bytes=MX_ALIGN)
+        nc.gpsimd.tensor_scalar(last_neg[:], wd_grouped[:, :, last], 1.0, 0.0, ALU.mult, ALU.add)
+        neg_planes.append(last_neg[:])
+        turn_neg(1, bank_of(last))
         for j in range(TILES):
-            gradient(j, j)
+            gradient(j, bank_of(j))
             if j < 2:
                 row_factor(j + 2)
         quantise_neg_along_i()
@@ -327,6 +342,6 @@ def tile_attend_gspos_sm_x_kernel(tc, x, wT, us, ts, wt, offs, poffs, out):
             positive_share(j)
             keep_positives(j)
         for j in range(TILES):
-            multiply(j, j)
+            multiply(j, bank_of(j))
         for j in range(TILES):
             finish(j, 2 if j == TILES - 1 else 1)

@@ -27,6 +27,7 @@ MX_ALIGN = 64
 ROOM = 2048
 RUN = 4
 ROUNDED_ON_SCALAR = 2
+EARLY = 2
 PADDED = SLOTS + 8
 
 LAST_PLANE_AT = 0
@@ -155,8 +156,8 @@ def tile_attend_gspos_sm_x_kernel(tc, x, wT, us, ts, wt, offs, poffs, out):
                 nc.tensor.transpose(turned[:, block(j)], ts_neg[:, column(j)].to_broadcast([P, P]), ident[:])
             nc.scalar.copy(ts_neg_spread[:], turned[:])
 
-        w_neg = keep.tile([P, PACK - 1, SLOTS], BF16, name="w_neg", align_bytes=MX_ALIGN)
-        neg_planes = [w_neg[:, t, :] for t in range(PACK - 1)]
+        w_neg = keep.tile([P, EARLY, SLOTS], BF16, name="w_neg", align_bytes=MX_ALIGN)
+        neg_planes = [w_neg[:, t, :] for t in range(EARLY)]
         wd_grouped = keep.tile([P, SLOTS, PACK], BF16, name="wd_grouped", align_bytes=MX_ALIGN)
         wd_codes = keep.tile([P, SLOTS], U32, name="wd_codes", align_bytes=MX_ALIGN)
         wd_scales = keep.tile([P, SLOTS], U8, name="wd_scales", align_bytes=MX_ALIGN)
@@ -165,12 +166,12 @@ def tile_attend_gspos_sm_x_kernel(tc, x, wT, us, ts, wt, offs, poffs, out):
         wi_scales = keep.tile([P, FEATURES], U8, name="wi_scales", align_bytes=MX_ALIGN)
 
         def gather_neg(t):
-            target = wd_grouped[:, :, t] if t == PACK - 1 else w_neg[:, t, :]
+            target = w_neg[:, t, :] if t < EARLY else wd_grouped[:, :, t]
             nc.vector.tensor_copy(target, planes[t][:].indirect(neg_list[:]))
 
         def group_early_planes():
             nc.vector.tensor_copy(
-                wd_grouped[:, :, 0:PACK - 1].rearrange("p (c i) t -> p c t i", i=RUN),
+                wd_grouped[:, :, 0:EARLY].rearrange("p (c i) t -> p c t i", i=RUN),
                 w_neg[:].rearrange("p t (c i) -> p c t i", i=RUN),
             )
 
@@ -302,11 +303,11 @@ def tile_attend_gspos_sm_x_kernel(tc, x, wT, us, ts, wt, offs, poffs, out):
             gather_neg(t)
             gather_pos(t)
             if t == 1:
+                group_early_planes()
                 turn_neg(0, 0)
                 for j in range(TILES):
                     load_x(j)
             turn_pos(t)
-        group_early_planes()
         gather_neg(last)
         gather_pos(last)
         quantise_neg_along_d()
@@ -329,9 +330,11 @@ def tile_attend_gspos_sm_x_kernel(tc, x, wT, us, ts, wt, offs, poffs, out):
             softmax(j, bank_of(j))
             if j >= 2:
                 row_factor(j - 2)
-        last_neg = keep.tile([P, SLOTS], BF16, name="last_neg", tag="x_grouped1", align_bytes=MX_ALIGN)
-        nc.gpsimd.tensor_scalar(last_neg[:], wd_grouped[:, :, last], 1.0, 0.0, ALU.mult, ALU.add)
-        neg_planes.append(last_neg[:])
+        late_neg = keep.tile([P, PACK - EARLY, SLOTS], BF16, name="late_neg", tag="x_grouped1", align_bytes=MX_ALIGN)
+        nc.gpsimd.tensor_scalar(
+            late_neg[:], wd_grouped[:, :, EARLY:PACK].rearrange("p c t -> p t c"), 1.0, 0.0, ALU.mult, ALU.add
+        )
+        neg_planes.extend(late_neg[:, a, :] for a in range(PACK - EARLY))
         turn_neg(1, bank_of(last))
         for j in range(TILES):
             gradient(j, bank_of(j))

@@ -26,7 +26,7 @@ LIST_ROWS = 16
 MX_ALIGN = 64
 ROOM = 2048
 RUN = 4
-ROUNDED_ON_SCALAR = 2
+ROUNDED_ON_SCALAR = (1, 2)
 EARLY = 2
 PADDED = SLOTS + 8
 
@@ -106,7 +106,7 @@ def tile_attend_gspos_sm_x_kernel(tc, x, wT, us, ts, wt, offs, poffs, out):
         def round_x(j):
             rounded = x_bf[j][:].rearrange("r (u p e) -> r u p e", u=2, e=2)
             rows = x_rows[j][:].rearrange("r (p u e) -> r u p e", u=2, e=2)
-            if j == ROUNDED_ON_SCALAR:
+            if j in ROUNDED_ON_SCALAR:
                 nc.scalar.activation(rounded, rows, ACT.Copy)
             else:
                 nc.gpsimd.tensor_scalar(rounded, rows, 1.0, 0.0, ALU.mult, ALU.add)
@@ -169,14 +169,20 @@ def tile_attend_gspos_sm_x_kernel(tc, x, wT, us, ts, wt, offs, poffs, out):
             target = w_neg[:, t, :] if t < EARLY else wd_grouped[:, :, t]
             nc.vector.tensor_copy(target, planes[t][:].indirect(neg_list[:]))
 
+        def gather_last_neg(h):
+            entries = neg_list[:, h * HALF // LIST_ROWS:(h + 1) * HALF // LIST_ROWS]
+            nc.vector.tensor_copy(wd_grouped[:, half(h), PACK - 1], planes[PACK - 1][:].indirect(entries))
+
         def group_early_planes():
             nc.vector.tensor_copy(
                 wd_grouped[:, :, 0:EARLY].rearrange("p (c i) t -> p c t i", i=RUN),
                 w_neg[:].rearrange("p t (c i) -> p c t i", i=RUN),
             )
 
-        def quantise_neg_along_d():
-            nc.vector.quantize_mx(out=wd_codes[:].bitcast(E4M3), scales=wd_scales[:], in_=flat(wd_grouped[:]))
+        def quantise_neg_along_d(h):
+            nc.vector.quantize_mx(
+                out=wd_codes[:, half(h)].bitcast(E4M3), scales=wd_scales[:, half(h)], in_=flat(wd_grouped[:, half(h), :])
+            )
 
         def turn_neg(m, number):
             wi_words = flat(wi_grouped[:]).bitcast(F32).rearrange("s (p t u) -> s p t u", t=PACK, u=2)
@@ -308,9 +314,11 @@ def tile_attend_gspos_sm_x_kernel(tc, x, wT, us, ts, wt, offs, poffs, out):
                 for j in range(TILES):
                     load_x(j)
             turn_pos(t)
-        gather_neg(last)
+        gather_last_neg(0)
+        gather_last_neg(1)
         gather_pos(last)
-        quantise_neg_along_d()
+        quantise_neg_along_d(0)
+        quantise_neg_along_d(1)
         turn_pos(last)
         for j in range(TILES):
             round_x(j)

@@ -35,6 +35,8 @@ TS_POS_AT = 0
 FIRST_PLANE_AT = 4 * ROOM
 X_AT = FIRST_PLANE_AT + 2 * ROOM
 MINUS_Z_AT = 12 * ROOM
+EARLY_NEG_AT = 17 * ROOM
+X_GROUPED_AT = 20 * ROOM
 
 
 def tile_attend_gspos_sm_x_kernel(tc, x, wT, us, ts, wt, offs, poffs, out):
@@ -97,8 +99,8 @@ def tile_attend_gspos_sm_x_kernel(tc, x, wT, us, ts, wt, offs, poffs, out):
 
         x_bf = [keep.tile([P, FEATURES], BF16, name=f"x_bf{j}", align_bytes=MX_ALIGN) for j in range(TILES)]
         x_grouped = [
-            keep.tile([P, HALF, PACK], BF16, name="x_grouped", tag=f"x_grouped{h}", align_bytes=MX_ALIGN)
-            for h in range(2)
+            keep.tile([P, HALF, PACK], BF16, name="x_grouped", tag="x_grouped0", align_bytes=MX_ALIGN),
+            shared.tile([P, HALF, PACK], BF16, name="x_grouped1", offset=X_GROUPED_AT, align_bytes=MX_ALIGN),
         ]
         x_codes = keep.tile([P, ROWS], U32, name="x_codes", align_bytes=MX_ALIGN)
         x_scales = keep.tile([P, ROWS], U8, name="x_scales", align_bytes=MX_ALIGN)
@@ -156,7 +158,7 @@ def tile_attend_gspos_sm_x_kernel(tc, x, wT, us, ts, wt, offs, poffs, out):
                 nc.tensor.transpose(turned[:, block(j)], ts_neg[:, column(j)].to_broadcast([P, P]), ident[:])
             nc.scalar.copy(ts_neg_spread[:], turned[:])
 
-        w_neg = keep.tile([P, EARLY, SLOTS], BF16, name="w_neg", align_bytes=MX_ALIGN)
+        w_neg = shared.tile([P, EARLY, SLOTS], BF16, name="w_neg", offset=EARLY_NEG_AT, align_bytes=MX_ALIGN)
         neg_planes = [w_neg[:, t, :] for t in range(EARLY)]
         wd_grouped = keep.tile([P, SLOTS, PACK], BF16, name="wd_grouped", align_bytes=MX_ALIGN)
         wd_codes = keep.tile([P, SLOTS], U32, name="wd_codes", align_bytes=MX_ALIGN)
@@ -267,7 +269,7 @@ def tile_attend_gspos_sm_x_kernel(tc, x, wT, us, ts, wt, offs, poffs, out):
 
         def gradient(j, number):
             nc.vector.scalar_tensor_tensor(
-                g[j][:], e[:, j, 0:SLOTS], inv[:, column(j)], wt_us_ts[:, j, :], ALU.mult, ALU.mult
+                g[j][:], e[:, j, 0:SLOTS], inv[:, column(j)], wt_us_ts[j], ALU.mult, ALU.mult
             )
             bank = bank_tile(number)
             words = g[j][:].bitcast(F32)
@@ -301,9 +303,6 @@ def tile_attend_gspos_sm_x_kernel(tc, x, wT, us, ts, wt, offs, poffs, out):
         last = PACK - 1
         factors()
         load_plane(last)
-        wt_us_ts = keep.tile([P, TILES, SLOTS], F32, name="wt_us_ts")
-        for j in range(TILES):
-            nc.gpsimd.tensor_scalar(wt_us_ts[:, j, :], ts_neg_spread[:], wt_us[:, column(j)], 0.0, ALU.mult, ALU.add)
         pos_banks = [bank_tile(TILES + j) for j in range(TILES)]
         for t in range(PACK - 1):
             gather_neg(t)
@@ -314,6 +313,15 @@ def tile_attend_gspos_sm_x_kernel(tc, x, wT, us, ts, wt, offs, poffs, out):
                 for j in range(TILES):
                     load_x(j)
             turn_pos(t)
+        early_factors = shared.tile([P, last, SLOTS], F32, name="early_factors", offset=EARLY_NEG_AT, align_bytes=MX_ALIGN)
+        last_factors = shared.tile([P, SLOTS], F32, name="last_factors", offset=X_GROUPED_AT + ROOM, align_bytes=MX_ALIGN)
+        wt_us_ts = [early_factors[:, j, :] for j in range(last)] + [last_factors[:]]
+
+        def column_factors(j):
+            nc.gpsimd.tensor_scalar(wt_us_ts[j], ts_neg_spread[:], wt_us[:, column(j)], 0.0, ALU.mult, ALU.add)
+
+        for j in range(last):
+            column_factors(j)
         gather_last_neg(0)
         gather_last_neg(1)
         gather_pos(last)
@@ -326,7 +334,7 @@ def tile_attend_gspos_sm_x_kernel(tc, x, wT, us, ts, wt, offs, poffs, out):
         quantise_x(1, 2)
         first_products = keep.tile([P, FEATURES], F32, name="first_products")
         second_products = keep.tile([P, FEATURES], F32, name="second_products", tag="x_grouped0", align_bytes=MX_ALIGN)
-        last_products = keep.tile([P, 2, FEATURES], F32, name="last_products", tag="x_grouped1", align_bytes=MX_ALIGN)
+        last_products = shared.tile([P, 2, FEATURES], F32, name="last_products", offset=X_GROUPED_AT, align_bytes=MX_ALIGN)
         products = [first_products[:], second_products[:], last_products[:, 0, :], last_products[:, 1, :]]
         scores(0, 0, 3)
         scores(1, 0, 0)
@@ -338,11 +346,12 @@ def tile_attend_gspos_sm_x_kernel(tc, x, wT, us, ts, wt, offs, poffs, out):
             softmax(j, bank_of(j))
             if j >= 2:
                 row_factor(j - 2)
-        late_neg = keep.tile([P, PACK - EARLY, SLOTS], BF16, name="late_neg", tag="x_grouped1", align_bytes=MX_ALIGN)
+        late_neg = shared.tile([P, PACK - EARLY, SLOTS], BF16, name="late_neg", offset=X_GROUPED_AT, align_bytes=MX_ALIGN)
         nc.gpsimd.tensor_scalar(
             late_neg[:], wd_grouped[:, :, EARLY:PACK].rearrange("p c t -> p t c"), 1.0, 0.0, ALU.mult, ALU.add
         )
         neg_planes.extend(late_neg[:, a, :] for a in range(PACK - EARLY))
+        column_factors(last)
         turn_neg(1, bank_of(last))
         for j in range(TILES):
             gradient(j, bank_of(j))

from contextlib import ExitStack

import concourse.mybir as mybir
from concourse.masks import make_identity

ROWS, FEATURES, ITEMS, SLOTS = 512, 512, 2048, 512
FLOPS = 2 * 2 * ROWS * FEATURES * SLOTS

F32 = mybir.dt.float32
BF16 = mybir.dt.bfloat16
U32 = mybir.dt.uint32
U16 = mybir.dt.uint16
U8 = mybir.dt.uint8
E4M3 = mybir.dt.float8_e4m3fn_x4
E5M2 = mybir.dt.float8_e5m2_x4
ALU = mybir.AluOpType
ACT = mybir.ActivationFunctionType

P = 128
PACK = 4
TILES = 4
HALF = 256
BANK = 512
LAST = P - 1
LIST_ROWS = 16
MX_ALIGN = 64
ROOM = 2048
RUN = 4
ROUNDED_ON_SCALAR = (1, 2)
EARLY = 2
PADDED = SLOTS + 8

LAST_PLANE_AT = 0
TS_POS_AT = 0
FIRST_PLANE_AT = 4 * ROOM
X_AT = FIRST_PLANE_AT + 2 * ROOM
MINUS_Z_AT = 12 * ROOM
EARLY_NEG_AT = 17 * ROOM
X_GROUPED_AT = 20 * ROOM


def tile_attend_gspos_sm_x_kernel(tc, x, wT, us, ts, wt, offs, poffs, out):
    nc = tc.nc
    with ExitStack() as ctx:
        keep = ctx.enter_context(tc.tile_pool(name="keep", bufs=1))
        shared = ctx.enter_context(tc.tile_pool(name="shared", bufs=1))
        psum = ctx.enter_context(tc.psum_pool(name="psum", bufs=1))

        def bank_tile(number):
            return psum.tile([P, BANK], F32, name="bank", tag=f"bank{number}")

        def block(j):
            return slice(j * P, (j + 1) * P)

        def half(h):
            return slice(h * HALF, (h + 1) * HALF)

        def column(j):
            return slice(j, j + 1)

        def flat(grouped):
            return grouped.rearrange("p c t -> p (c t)")

        neg_list = keep.tile([P, SLOTS // LIST_ROWS], U16, name="neg_list")
        pos_list = keep.tile([P, ROWS // LIST_ROWS], U16, name="pos_list")
        ts_table = keep.tile([P, ITEMS], F32, name="ts_table")
        row_factors = keep.tile([P, ROWS], F32, name="row_factors")
        planes = [
            shared.tile([P, ITEMS], F32, name="plane0", offset=FIRST_PLANE_AT, align_bytes=MX_ALIGN),
            shared.tile([P, ITEMS], F32, name="plane1", offset=FIRST_PLANE_AT + 4 * ROOM, align_bytes=MX_ALIGN),
            keep.tile([P, ITEMS], F32, name="plane2"),
            shared.tile([P, ITEMS], F32, name="plane3", offset=LAST_PLANE_AT, align_bytes=MX_ALIGN),
        ]
        x_rows = [
            shared.tile([P, FEATURES], F32, name=f"x_rows{j}", offset=X_AT + j * ROOM, align_bytes=MX_ALIGN)
            for j in range(TILES)
        ]
        ident = keep.tile([P, P], F32, name="ident")

        wT_planes = wT.rearrange("(p t) c -> t p c", t=PACK)
        nc.sync.dma_start(ts_table[LAST:P, :], ts[0:1, :])
        nc.sync.dma_start(neg_list[:], offs)
        nc.sync.dma_start(pos_list[:], poffs)

        def load_plane(t):
            nc.sync.dma_start(planes[t][:], wT_planes[t])

        def load_x(j):
            nc.sync.dma_start(x_rows[j][:], x[block(j), :])

        load_plane(0)
        nc.sync.dma_start(row_factors[LAST - 1:LAST, :], us.rearrange("r o -> o r"))
        nc.sync.dma_start(row_factors[LAST:P, :], wt.rearrange("r o -> o r"))
        load_plane(1)
        load_plane(2)
        nc.vector.memset(ts_table[0:LAST, :], 0.0)
        make_identity(nc, ident[:])
        nc.gpsimd.memset(row_factors[0:LAST - 1, :], 0.0)

        x_bf = [keep.tile([P, FEATURES], BF16, name=f"x_bf{j}", align_bytes=MX_ALIGN) for j in range(TILES)]
        x_grouped = [
            keep.tile([P, HALF, PACK], BF16, name="x_grouped", tag="x_grouped0", align_bytes=MX_ALIGN),
            shared.tile([P, HALF, PACK], BF16, name="x_grouped1", offset=X_GROUPED_AT, align_bytes=MX_ALIGN),
        ]
        x_codes = keep.tile([P, ROWS], U32, name="x_codes", align_bytes=MX_ALIGN)
        x_scales = keep.tile([P, ROWS], U8, name="x_scales", align_bytes=MX_ALIGN)

        def round_x(j):
            rounded = x_bf[j][:].rearrange("r (u p e) -> r u p e", u=2, e=2)
            rows = x_rows[j][:].rearrange("r (p u e) -> r u p e", u=2, e=2)
            if j in ROUNDED_ON_SCALAR:
                nc.scalar.activation(rounded, rows, ACT.Copy)
            else:
                nc.gpsimd.tensor_scalar(rounded, rows, 1.0, 0.0, ALU.mult, ALU.add)

        def quantise_x(h, number):
            bank = bank_tile(number)
            for a in range(2):
                words = x_bf[2 * h + a][:].bitcast(F32)
                for u in range(2):
                    nc.tensor.transpose(bank[:, block(2 * a + u)], words[:, block(u)], ident[:])
            nc.scalar.copy(
                flat(x_grouped[h][:]).bitcast(F32).rearrange("p (a r u) -> p a r u", a=2, u=2),
                bank[:].rearrange("p (a u r) -> p a r u", a=2, u=2),
            )
            nc.vector.quantize_mx(out=x_codes[:, half(h)].bitcast(E4M3), scales=x_scales[:, half(h)], in_=flat(x_grouped[h][:]))

        def turn_rows(rows, number):
            bank = bank_tile(number)
            for j in range(TILES):
                nc.tensor.transpose(bank[:, block(j)], rows[:, block(j)], ident[:])
            return bank

        ts_neg_row = keep.tile([P, SLOTS], F32, name="ts_neg_row")
        ts_pos_row = shared.tile([P, ROWS], F32, name="ts_pos_row", offset=TS_POS_AT, align_bytes=MX_ALIGN)
        ts_neg = keep.tile([P, TILES], F32, name="ts_neg")
        ts_neg_spread = keep.tile([P, SLOTS], F32, name="ts_neg_spread")
        us_col = keep.tile([P, TILES], F32, name="us_col")
        minus_us = keep.tile([P, TILES], F32, name="minus_us")
        wt_us = keep.tile([P, TILES], F32, name="wt_us")
        minus_us_tp = keep.tile([P, TILES], F32, name="minus_us_tp")
        wt_us_tp = keep.tile([P, TILES], F32, name="wt_us_tp")

        def factors():
            nc.vector.tensor_copy(ts_neg_row[:], ts_table[:].indirect(neg_list[:]))
            nc.vector.tensor_copy(ts_pos_row[:], ts_table[:].indirect(pos_list[:]))
            turned = turn_rows(row_factors, 0)
            nc.vector.tensor_copy(us_col[:], turned[:, LAST - 1::P])
            nc.vector.tensor_scalar(minus_us[:], turned[:, LAST - 1::P], -1.0, None, ALU.mult)
            nc.vector.tensor_tensor(wt_us[:], turned[:, LAST::P], us_col[:], ALU.mult)
            turned = turn_rows(ts_neg_row, 1)
            nc.vector.tensor_copy(ts_neg[:], turned[:, LAST::P])
            turned = turn_rows(ts_pos_row, 2)
            nc.vector.tensor_tensor(minus_us_tp[:], turned[:, LAST::P], minus_us[:], ALU.mult)
            nc.vector.tensor_tensor(wt_us_tp[:], turned[:, LAST::P], wt_us[:], ALU.mult)
            turned = bank_tile(3)
            for j in range(TILES):
                nc.tensor.transpose(turned[:, block(j)], ts_neg[:, column(j)].to_broadcast([P, P]), ident[:])
            nc.scalar.copy(ts_neg_spread[:], turned[:])

        w_neg = shared.tile([P, EARLY, SLOTS], BF16, name="w_neg", offset=EARLY_NEG_AT, align_bytes=MX_ALIGN)
        neg_planes = [w_neg[:, t, :] for t in range(EARLY)]
        wd_grouped = keep.tile([P, SLOTS, PACK], BF16, name="wd_grouped", align_bytes=MX_ALIGN)
        wd_codes = keep.tile([P, SLOTS], U32, name="wd_codes", align_bytes=MX_ALIGN)
        wd_scales = keep.tile([P, SLOTS], U8, name="wd_scales", align_bytes=MX_ALIGN)
        wi_grouped = keep.tile([P, FEATURES, PACK], BF16, name="wi_grouped", align_bytes=MX_ALIGN)
        wi_codes = keep.tile([P, FEATURES], U32, name="wi_codes", align_bytes=MX_ALIGN)
        wi_scales = keep.tile([P, FEATURES], U8, name="wi_scales", align_bytes=MX_ALIGN)

        def gather_neg(t):
            target = w_neg[:, t, :] if t < EARLY else wd_grouped[:, :, t]
            nc.vector.tensor_copy(target, planes[t][:].indirect(neg_list[:]))

        def gather_last_neg(h):
            entries = neg_list[:, h * HALF // LIST_ROWS:(h + 1) * HALF // LIST_ROWS]
            nc.vector.tensor_copy(wd_grouped[:, half(h), PACK - 1], planes[PACK - 1][:].indirect(entries))

        def group_early_planes():
            nc.vector.tensor_copy(
                wd_grouped[:, :, 0:EARLY].rearrange("p (c i) t -> p c t i", i=RUN),
                w_neg[:].rearrange("p t (c i) -> p c t i", i=RUN),
            )

        def quantise_neg_along_d(h):
            nc.vector.quantize_mx(
                out=wd_codes[:, half(h)].bitcast(E4M3), scales=wd_scales[:, half(h)], in_=flat(wd_grouped[:, half(h), :])
            )

        def turn_neg(m, number):
            wi_words = flat(wi_grouped[:]).bitcast(F32).rearrange("s (p t u) -> s p t u", t=PACK, u=2)
            bank = bank_tile(number)
            for a in reversed(range(2)):
                for u in range(2):
                    nc.tensor.transpose(bank[:, block(2 * a + u)], neg_planes[2 * m + a].bitcast(F32)[:, u::2], ident[:])
            nc.scalar.copy(wi_words[:, :, 2 * m:2 * m + 2, :], bank[:].rearrange("s (a u p) -> s p a u", a=2, u=2))

        def quantise_neg_along_i():
            nc.vector.quantize_mx(out=wi_codes[:].bitcast(E4M3), scales=wi_scales[:], in_=flat(wi_grouped[:]))

        w_pos = [keep.tile([P, ROWS], F32, name=f"w_pos{t}") for t in range(PACK)]
        w_pos_rows = {}
        minus_z = shared.tile([P, TILES, PADDED], F32, name="minus_z", offset=MINUS_Z_AT, align_bytes=MX_ALIGN)
        e = keep.tile([P, TILES, PADDED], F32, name="e")
        minus_m = keep.tile([P, TILES], F32, name="minus_m")
        tot = keep.tile([P, TILES], F32, name="tot")
        inv = keep.tile([P, TILES], F32, name="inv")
        pos_share = keep.tile([P, TILES], F32, name="pos_share")

        def gather_pos(t):
            nc.scalar.activation(w_pos[t][:], planes[t][:].indirect(pos_list[:]), ACT.Copy)

        def turn_pos(t):
            for j in range(TILES):
                nc.tensor.transpose(pos_banks[j][:, t::PACK], w_pos[t][:, block(j)], ident[:])

        def positive_score(j, products):
            nc.vector.scalar_tensor_tensor(
                products, pos_banks[j][:], minus_us_tp[:, column(j)], x_rows[j][:], ALU.mult, ALU.mult,
                accum_out=minus_z[:, j, column(SLOTS)],
            )

        def keep_positives(j):
            w_pos_rows[j] = shared.tile(
                [P, FEATURES], F32, name=f"w_pos_rows{j}", offset=MINUS_Z_AT + j * ROOM, align_bytes=MX_ALIGN
            )
            nc.scalar.mul(w_pos_rows[j][:], pos_banks[j][:], wt_us_tp[:, column(j)])

        scaled = [keep.tile([P, TILES, HALF], F32, name=f"scaled{r}") for r in range(2)]

        def scores(h, rows, number):
            bank = bank_tile(number)
            for n in range(2):
                slots = block(2 * h + n)
                nc.tensor.matmul_mx(
                    out=bank[:, half(n)], lhsT=wd_codes[:, slots].bitcast(E4M3), lhsT_scale=wd_scales[:, slots],
                    rhs=x_codes[:, half(rows)].bitcast(E4M3), rhs_scale=x_scales[:, half(rows)], start=True, stop=True,
                )
            for n in range(2):
                s = 2 * h + n
                nc.scalar.activation(scaled[rows][:, s, :], bank[:, half(n)], ACT.Copy, scale=ts_neg[:, column(s)])

        def softmax(j, number):
            bank = bank_tile(number)
            for s in range(TILES):
                nc.tensor.transpose(bank[:, block(s)], scaled[j // 2][:, s, block(j % 2)], ident[:])
            nc.vector.tensor_scalar(
                minus_z[:, j, 0:SLOTS], bank[:], minus_us[:, column(j)], minus_z[:, j, column(SLOTS)], ALU.mult, ALU.min,
                accum_out=minus_m[:, column(j)],
            )
            nc.scalar.activation(
                e[:, j, 0:SLOTS + 1], minus_z[:, j, 0:SLOTS + 1], ACT.Exp, bias=minus_m[:, column(j)], scale=-1.0,
                accum_out=tot[:, column(j)],
            )

        def row_factor(j):
            nc.vector.reciprocal(inv[:, column(j)], tot[:, column(j)])

        def positive_share(j):
            nc.scalar.activation(
                pos_share[:, column(j)], e[:, j, column(SLOTS)], ACT.Identity, scale=inv[:, column(j)], bias=-1.0
            )

        g = [keep.tile([P, SLOTS], BF16, name=f"g{j}", align_bytes=MX_ALIGN) for j in range(TILES)]
        g_grouped = [keep.tile([P, P, PACK], BF16, name=f"g_grouped{j}", align_bytes=MX_ALIGN) for j in range(TILES)]
        g_codes = [keep.tile([P, P], U32, name=f"g_codes{j}", align_bytes=MX_ALIGN) for j in range(TILES)]
        g_scales = [keep.tile([P, P], U8, name=f"g_scales{j}", align_bytes=MX_ALIGN) for j in range(TILES)]
        result = [keep.tile([P, FEATURES], F32, name=f"result{j}") for j in range(TILES)]
        gx = {}

        def gradient(j, number):
            nc.vector.scalar_tensor_tensor(
                g[j][:], e[:, j, 0:SLOTS], inv[:, column(j)], wt_us_ts[j], ALU.mult, ALU.mult
            )
            bank = bank_tile(number)
            words = g[j][:].bitcast(F32)
            for u in range(2):
                nc.tensor.transpose(bank[:, block(u)], words[:, u::2], ident[:])
            nc.scalar.copy(
                flat(g_grouped[j][:]).bitcast(F32).rearrange("p (r u) -> p r u", u=2),
                bank[:, 0:HALF].rearrange("p (u r) -> p r u", u=2),
            )

        def multiply(j, number):
            nc.vector.quantize_mx(out=g_codes[j][:].bitcast(E5M2), scales=g_scales[j][:], in_=flat(g_grouped[j][:]))
            gx[j] = bank_tile(number)
            nc.tensor.matmul_mx(
                out=gx[j][:], lhsT=g_codes[j][:].bitcast(E5M2), lhsT_scale=g_scales[j][:],
                rhs=wi_codes[:].bitcast(E4M3), rhs_scale=wi_scales[:], start=True, stop=True,
            )

        def finish(j, pieces):
            width = FEATURES // pieces
            for n in range(pieces):
                cols = slice(n * width, (n + 1) * width)
                nc.vector.scalar_tensor_tensor(
                    result[j][:, cols], w_pos_rows[j][:, cols], pos_share[:, column(j)], gx[j][:, cols], ALU.mult, ALU.add
                )
                nc.sync.dma_start(out[block(j), cols], result[j][:, cols])

        def bank_of(j):
            return (j + 3) % TILES

        last = PACK - 1
        factors()
        load_plane(last)
        pos_banks = [bank_tile(TILES + j) for j in range(TILES)]
        for t in range(PACK - 1):
            gather_neg(t)
            gather_pos(t)
            if t == 1:
                group_early_planes()
                turn_neg(0, 0)
                for j in range(TILES):
                    load_x(j)
            turn_pos(t)
        early_factors = shared.tile([P, last, SLOTS], F32, name="early_factors", offset=EARLY_NEG_AT, align_bytes=MX_ALIGN)
        last_factors = shared.tile([P, SLOTS], F32, name="last_factors", offset=X_GROUPED_AT + ROOM, align_bytes=MX_ALIGN)
        wt_us_ts = [early_factors[:, j, :] for j in range(last)] + [last_factors[:]]

        def column_factors(j):
            nc.gpsimd.tensor_scalar(wt_us_ts[j], ts_neg_spread[:], wt_us[:, column(j)], 0.0, ALU.mult, ALU.add)

        for j in range(last):
            column_factors(j)
        gather_last_neg(0)
        gather_last_neg(1)
        gather_pos(last)
        quantise_neg_along_d(0)
        quantise_neg_along_d(1)
        turn_pos(last)
        for j in range(TILES):
            round_x(j)
        quantise_x(0, 1)
        quantise_x(1, 2)
        first_products = keep.tile([P, FEATURES], F32, name="first_products")
        second_products = keep.tile([P, FEATURES], F32, name="second_products", tag="x_grouped0", align_bytes=MX_ALIGN)
        last_products = shared.tile([P, 2, FEATURES], F32, name="last_products", offset=X_GROUPED_AT, align_bytes=MX_ALIGN)
        products = [first_products[:], second_products[:], last_products[:, 0, :], last_products[:, 1, :]]
        scores(0, 0, 3)
        scores(1, 0, 0)
        scores(0, 1, 1)
        scores(1, 1, 2)
        for j in range(TILES):
            positive_score(j, products[j])
        for j in range(TILES):
            softmax(j, bank_of(j))
            if j >= 2:
                row_factor(j - 2)
        late_neg = shared.tile([P, PACK - EARLY, SLOTS], BF16, name="late_neg", offset=X_GROUPED_AT, align_bytes=MX_ALIGN)
        nc.gpsimd.tensor_scalar(
            late_neg[:], wd_grouped[:, :, EARLY:PACK].rearrange("p c t -> p t c"), 1.0, 0.0, ALU.mult, ALU.add
        )
        neg_planes.extend(late_neg[:, a, :] for a in range(PACK - EARLY))
        column_factors(last)
        turn_neg(1, bank_of(last))
        for j in range(TILES):
            gradient(j, bank_of(j))
            if j < 2:
                row_factor(j + 2)
        quantise_neg_along_i()
        for j in range(TILES):
            positive_share(j)
            keep_positives(j)
        for j in range(TILES):
            multiply(j, bank_of(j))
        for j in range(TILES):
            finish(j, 2 if j == TILES - 1 else 1)
